import numpy as np, ml_dtypes
CORES = [5,29,101,125,133,157,229,253]
N = 8
BF = ml_dtypes.bfloat16
def gentries(a):
    return np.ascontiguousarray(a.reshape(8, 16, -1).transpose(0, 2, 1)).reshape(8, -1)
def gtable(e):
    e = np.asarray(e); return np.ascontiguousarray(e.reshape(8, -1, 16).transpose(0, 2, 1)).reshape(128, -1).astype(np.int32)
W, n, V, C, Z = 6, 2048, 8192, 1024, 256
def counts(rng, h, z):
    c = np.zeros((N, 8, W), np.int64)
    for r in range(N):
        for g in range(8):
            m = int(h[r, g] - z[r, g]) - (W - 2); b = np.sort(rng.integers(0, m + 1, W - 3))
            c[r, g, 0] = n - h[r, g]; c[r, g, 1:W - 1] = np.diff(np.concatenate([[0], b, [m]])) + 1; c[r, g, W - 1] = z[r, g]
    return c
def some(rng):
    return rng.integers(C - C // 4, C + 1, (N, 8)), rng.integers(Z // 2, Z + 1, (N, 8))
def names(rng):
    return np.stack([np.stack([rng.permutation(V)[:n] for g in range(8)]) for r in range(N)]).astype(np.int64)
def depths(rng, c):
    return np.stack([np.stack([rng.permutation(np.repeat(np.arange(W), c[r, g])) for g in range(8)]) for r in range(N)])
def link(rng, o, dep):
    x = np.zeros((N, 8, n), np.int64)
    for r in range(N):
        q = (r + 1) % N
        for g in range(8):
            m = np.ones(V, bool); m[o[q, g]] = False; free = np.flatnonzero(m)
            v = free[rng.integers(0, len(free), n)]
            for k in range(1, W):
                i = np.flatnonzero(dep[r, g] == k)
                if len(i):
                    t = np.flatnonzero(dep[q, g] == k - 1 if k < W - 1 else dep[q, g] >= W - 2)
                    v[i] = o[q, g][t[rng.integers(0, len(t), len(i))]]
            x[r, g] = v
    return x
def pack(o, x, s):
    return {"own": np.stack([gtable(a) for a in o]), "nxt": np.stack([gtable(a) for a in x]), "pts": np.asarray(s).astype(np.int32)}
def points(rng):
    return rng.integers(0, 256, (N, 8, n))
def setup_inputs(rng):
    h, z = some(rng); o = names(rng); dep = depths(rng, counts(rng, h, z))
    return pack(o, link(rng, o, dep), points(rng))
def setup_inputs_full(rng):
    o = names(rng); c = counts(rng, np.full((N, 8), C), np.full((N, 8), Z)); e = rng.permutation(8)[:4]
    c[:, e, 1:W - 2] = 1; c[:, e, W - 2] = C - Z - (W - 3)
    dep = depths(rng, c)
    return pack(o, link(rng, o, dep), points(rng))
def setup_inputs_few(rng):
    h, z = some(rng); e = rng.permutation(8); q = int(rng.integers(0, N)); o = names(rng)
    z[:, e[2]] = 1; z[:, e[3]] = np.where(rng.random(N) < 0.5, 0, z[:, e[3]]); z[q, e[3]] = 0; z[:, e[4]] = Z; h[:, e[4]] = C
    c = counts(rng, h, z); c[:, e[0], 0] = n; c[:, e[0], 1:] = 0
    for t in range(W - 1):
        r = (q - t) % N; c[r, e[1], 0] += np.sum(c[r, e[1], t + 1:]); c[r, e[1], t + 1:] = 0
    dep = depths(rng, c)
    return pack(o, link(rng, o, dep), points(rng))
def setup_inputs_repeats(rng):
    h, z = some(rng); o = names(rng); dep = depths(rng, counts(rng, h, z)); x = link(rng, o, dep)
    for r in range(N):
        for g in range(8):
            for k in (0, W - 1):
                i = np.flatnonzero(dep[r, g] == k); x[r, g, i] = x[r, g, i[0]]
    return pack(o, x, points(rng))
def setup_inputs_ends(rng):
    h, z = some(rng); dep = depths(rng, counts(rng, h, z))
    o = 1 + np.stack([np.stack([rng.permutation(V - 2)[:n] for g in range(8)]) for r in range(N)]).astype(np.int64)
    for r in range(N):
        for g in range(0, 8, 2):
            o[r, g, 0] = 0; o[r, g, n - 1] = V - 1; a = dep[r, g]
            i = np.flatnonzero(a == W - 1); j = i[rng.integers(0, len(i))]; u, v = int(a[0]), int(a[j]); a[j] = u; a[0] = v
            i = np.flatnonzero(a[1:] == W - 1) + 1; j = i[rng.integers(0, len(i))]; u, v = int(a[n - 1]), int(a[j]); a[j] = u; a[n - 1] = v
    x = link(rng, o, dep)
    x[:, 0::2, 0] = V - 1; x[:, 0::2, n - 1] = 0
    for g in range(1, 8, 2):
        m = (dep[:, g] == 0) & (rng.random((N, n)) < 0.5)
        x[:, g] = np.where(m, rng.integers(0, 2, (N, n)) * (V - 1), x[:, g])
    return pack(o, x, 255 * rng.integers(0, 2, (N, 8, n)))
def setup_inputs_spread(rng):
    z = np.maximum(Z >> rng.integers(0, 7, (N, 8)), 1); h = z + np.maximum((C - Z) >> rng.integers(0, 7, (N, 8)), W - 2)
    o = np.stack([np.stack([(rng.integers(0, V) + rng.permutation(n + n // 8)[:n]) % V for g in range(8)]) for r in range(N)]).astype(np.int64)
    o[:, 1::2] = np.sort(o[:, 1::2], axis=2)
    dep = depths(rng, counts(rng, h, z))
    return pack(o, link(rng, o, dep), 255 >> rng.integers(0, 9, (N, 8, n)))
def followers(o, x):
    to = np.zeros((N, 8, n), np.int64)
    for r in range(N):
        for g in range(8):
            where = np.full(V, -1, np.int64); where[o[(r + 1) % N, g]] = np.arange(n); to[r, g] = where[x[r, g]]
    return to
def step(p, v, t):
    return np.take_along_axis(np.roll(v, -t, axis=0), p, axis=2)
def chains(to, s):
    p = np.broadcast_to(np.arange(n), (N, 8, n)); tot = s.astype(np.int64)
    for t in range(1, W):
        p = np.where(p >= 0, step(np.maximum(p, 0), to, t - 1), -1)
        tot = tot + np.where(p >= 0, step(np.maximum(p, 0), s, t), 0)
    return p, tot
def check_inputs(d):
    try:
        o = np.stack([gentries(a) for a in d["own"]]).astype(np.int64); x = np.stack([gentries(a) for a in d["nxt"]]).astype(np.int64); s = np.asarray(d["pts"]).astype(np.int64)
        if o.shape != (N, 8, n) or x.shape != (N, 8, n) or s.shape != (N, 8, n): return ["shapes"]
        bad = []
        if s.min() < 0 or s.max() > 255: bad.append("points")
        if o.min() < 0 or o.max() >= V or x.min() < 0 or x.max() >= V: return bad + ["names in range"]
        if (np.diff(np.sort(o, axis=2), axis=2) == 0).any(): return bad + ["own names differ"]
        to = followers(o, x); p, tot = chains(to, s)
        if np.max(np.count_nonzero(to >= 0, axis=2)) > C: bad.append("followers")
        if np.max(np.count_nonzero(p >= 0, axis=2)) > Z: bad.append("kept")
        return bad
    except Exception:
        return ["shapes"]
def reference(own, nxt, pts):
    o = np.stack([gentries(a) for a in own]).astype(np.int64); x = np.stack([gentries(a) for a in nxt]).astype(np.int64)
    p, tot = chains(followers(o, x), pts)
    yk = np.full((N, 8, Z), -1, np.float32); ys = np.zeros((N, 8, Z), np.float32)
    for r in range(N):
        for g in range(8):
            i = np.flatnonzero(p[r, g] >= 0)
            yk[r, g, :len(i)] = o[r, g, i]; ys[r, g, :len(i)] = tot[r, g, i]
    return {"yk": yk, "ys": ys}

@@ -1,0 +1,403 @@
+from concourse.bass import DstId, RemoteDMATransfer
+from concourse.mybir import AluOpType as OP, ActivationFunctionType as AF
+
+SCRATCH = {
+    "nx": ("sbuf", [128, 128], "uint16"),
+    "rln": ("sbuf", [128, 128], "uint16"), "rlf": ("sbuf", [128, 128], "uint16"), "rlp": ("sbuf", [128, 128], "bfloat16"),
+    "owi": ("sbuf", [128, 128], "int32"), "nxi": ("sbuf", [128, 128], "int32"), "pti": ("sbuf", [128, 128], "int32"),
+    "own16": ("sbuf", [128, 128], "uint16"), "nxt16": ("sbuf", [128, 128], "uint16"), "pt0": ("sbuf", [128, 128], "bfloat16"),
+    "tab": ("sbuf", [128, 8192], "bfloat16"), "vr": ("sbuf", [128, 2048], "bfloat16"), "gr": ("sbuf", [128, 2048], "bfloat16"),
+    "f0": ("sbuf", [128, 128], "uint16"),
+    "wa": ("sbuf", [128, 2064], "bfloat16"), "wb": ("sbuf", [128, 2064], "bfloat16"), "rr": ("sbuf", [128, 2048], "bfloat16"),
+    "lo": ("sbuf", [128, 256], "bfloat16"), "m1": ("sbuf", [128, 256], "bfloat16"), "ip": ("sbuf", [128, 2], "int32"),
+    "io8": ("sbuf", [128, 8], "float32"), "pb": ("sbuf", [128, 1], "int32"), "ps": ("sbuf", [128, 1], "int32"),
+    "pg": ("sbuf", [128, 1], "int32"),
+    "ml": ("sbuf", [128, 1], "float32"), "nml": ("sbuf", [128, 1], "float32"), "hb": ("sbuf", [128, 8], "float32"),
+    "sf": ("sbuf", [128, 1], "float32"), "mk": ("sbuf", [128, 8], "float32"), "gf": ("sbuf", [128, 1], "float32"),
+    "ngf": ("sbuf", [128, 1], "float32"),
+    "zz": ("sbuf", [128, 160], "bfloat16"), "on": ("sbuf", [128, 160], "bfloat16"), "half": ("sbuf", [128, 32], "bfloat16"),
+    "basef": ("sbuf", [128, 144], "bfloat16"), "bases": ("sbuf", [128, 144], "bfloat16"), "ids": ("sbuf", [128, 160], "bfloat16"),
+    "bo": ("sbuf", [128, 128], "bfloat16"), "tri": ("sbuf", [128, 128], "bfloat16"), "bo16": ("sbuf", [128, 128], "bfloat16"),
+    "bo32": ("sbuf", [128, 8], "float32"), "kc": ("sbuf", [128, 128], "bfloat16"), "cp": ("sbuf", [128, 128], "bfloat16"),
+    "ck": ("sbuf", [128, 128], "bfloat16"), "msk": ("sbuf", [128, 32], "float32"),
+    "loi": ("sbuf", [128, 128], "int32"), "nlo": ("sbuf", [128, 144], "bfloat16"), "nhi": ("sbuf", [128, 144], "bfloat16"),
+    "kt": ("sbuf", [128, 128], "bfloat16"), "sc1": ("sbuf", [128, 144], "bfloat16"), "sumw": ("sbuf", [128, 144], "float32"),
+    "posk": ("sbuf", [128, 144], "bfloat16"), "ai": ("sbuf", [128, 128], "int32"), "a1": ("sbuf", [128, 128], "bfloat16"),
+    "bb": ("sbuf", [128, 128], "bfloat16"), "sg": ("sbuf", [128, 128], "bfloat16"), "cmm": ("sbuf", [128, 32], "float32"),
+    "lf": ("sbuf", [128, 16], "float32"), "lst": ("sbuf", [128, 16], "uint16"), "oh": ("sbuf", [128, 256], "bfloat16"),
+    "vs": ("sbuf", [128, 256], "float32"), "vh": ("sbuf", [128, 256], "bfloat16"), "vl": ("sbuf", [128, 256], "bfloat16"),
+    "yks": ("sbuf", [128, 256], "float32"), "yss": ("sbuf", [128, 256], "float32"),
+    "psa": ("psum", [128, 2048], "float32"), "pwa": ("psum", [128, 512], "float32"), "pwb": ("psum", [128, 512], "float32"),
+    "px": ("psum", [128, 512], "float32"), "py": ("psum", [128, 512], "float32"),
+}
+for _k in range(1, 6):
+    SCRATCH["f%d" % _k] = ("sbuf", [128, 128], "uint16")
+    SCRATCH["pt%d" % _k] = ("sbuf", [128, 128], "bfloat16")
+for _k in range(5):
+    SCRATCH["pr%d" % _k] = ("sbuf", [128, 2048], "bfloat16")
+NTOK = 126
+SEMAPHORES = (["t%d" % _k for _k in range(NTOK)] + ["anx", "rn", "rf", "rp", "lc"]
+              + ["af%d" % _k for _k in range(1, 6)] + ["ap%d" % _k for _k in range(1, 6)])
+
+ODD, EVEN = (5, 3, 1), (4, 2)
+
+
+def engs(topo, src, dst, a, b):
+    e = topo.engines(src, dst)[a:b]
+    return sum(1 << x for x in e), len(e)
+
+
+def write(g, T, topo, src, dst, out, in_, sem, a=0, b=8):
+    rid, pid = topo.addr(dst, src)
+    m, k = engs(topo, src, dst, a, b)
+    g.remote_dma(out, in_, T.sem[sem], T.sem["lc"], pid, rid, m)
+    return k
+
+
+def writes(g, T, topo, src, parts):
+    tr, n = [], 0
+    for dst, out, in_, sem, a, b in parts:
+        rid, pid = topo.addr(dst, src)
+        m, k = engs(topo, src, dst, a, b)
+        n += k
+        tr.append(RemoteDMATransfer(dst_ids=[DstId(rid=rid, pnc=pid)], dma_engine_mask=m, remote_sem=T.sem[sem], src=in_, dst=out))
+    g.remote_dma_fused(tr, local_sem=T.sem["lc"])
+    return n
+
+
+def helpers(T, topo, rc):
+    q, N = T.rank_of(rc), len(T.cores)
+    far = [T.cores[(q + 1) % N]] + [T.cores[(q - k) % N] for k in ODD]
+    c = [x for x in topo.cores_of(rc) if x != rc and topo.die(x) == topo.die(rc) and all(topo.may_write(x, d) for d in far)]
+    return c[0], c[1]
+
+
+def hand_on(g, core, T, topo):
+    N = len(T.cores)
+    for rc in T.cores:
+        if rc not in topo.cores_of(core):
+            continue
+        q = T.rank_of(rc)
+        A, B = helpers(T, topo, rc)
+        sent = 0
+        if core == A:
+            g.wait_ge(T.sem["rn"], 8)
+            sent += write(g, T, topo, core, T.cores[(q + 1) % N], T["nx"][:], T["rln"][:], "anx")
+            g.wait_ge(T.sem["rf"], 8)
+            sent += write(g, T, topo, core, T.cores[(q - 5) % N], T["f5"][:], T["rlf"][:], "af5")
+            sent += writes(g, T, topo, core, [(T.cores[(q - 3) % N], T["f3"][:], T["rlf"][:], "af3", 0, 4),
+                                              (T.cores[(q - 1) % N], T["f1"][:], T["rlf"][:], "af1", 4, 8)])
+        elif core == B:
+            g.wait_ge(T.sem["rp"], 8)
+            sent += writes(g, T, topo, core, [(T.cores[(q - 5) % N], T["pt5"][:], T["rlp"][:], "ap5", 0, 4),
+                                              (T.cores[(q - 3) % N], T["pt3"][:], T["rlp"][:], "ap3", 4, 6),
+                                              (T.cores[(q - 1) % N], T["pt1"][:], T["rlp"][:], "ap1", 6, 8)])
+        if sent:
+            g.wait_ge(T.sem["lc"], sent)
+
+
+AF_ENG = {5: 8, 4: 4, 3: 4, 2: 4, 1: 4}
+AP_ENG = {5: 4, 4: 4, 3: 2, 2: 4, 1: 2}
+
+
+def rank_program(g, core, T, topo):
+    q = T.rank_of(core)
+    if q is None:
+        hand_on(g, core, T, topo)
+        return
+    N = len(T.cores)
+    Q = {"g": g, "v": g.vector, "s": g.scalar, "t": g.tensor, "y": g.sync}
+    v, s, t = g.vector, g.scalar, g.tensor
+    used, seen = [0], {}
+
+    def tok():
+        used[0] += 1
+        return [T.sem["t%d" % (used[0] - 1)], 0, used[0] - 1]
+
+    def inc(op, k=None, n=1):
+        k = k or tok()
+        op.then_inc(k[0], n)
+        k[1] += n
+        return k
+
+    def W(queue, *toks):
+        for k in toks:
+            if seen.get((queue, k[2]), -1) < k[1]:
+                seen[(queue, k[2])] = k[1]
+                Q[queue].wait_ge(k[0], k[1])
+
+    def R(queue, sem, n):
+        if (queue, sem) not in seen:
+            seen[(queue, sem)] = n
+            Q[queue].wait_ge(T.sem[sem], n)
+
+    l_nx = inc(g.sync.dma_start(T["nxi"][:], T.nxt[:]), None, 16)
+    l_ow = inc(g.scalar.dma_start(T["owi"][:], T.own[:]), None, 16)
+    l_pt = inc(g.sync.dma_start(T["pti"][:], T.pts[:]), None, 16)
+
+    tab = T["tab"]
+    k_i = inc(g.iota(T["ip"][:, 0:1], [[0, 1]], 0, 1))
+    inc(g.iota(T["io8"][:], [[1, 8]], 0, 0, allow_small_or_imprecise_dtypes=True), k_i)
+    k_lo = inc(g.iota(T["lo"][:], [[1, 256]], 0, 0, allow_small_or_imprecise_dtypes=True))
+    GF = 768
+    k_fill = inc(g.iota(tab[:, 8192 - GF:8192], [[0, GF]], 8, 0, allow_small_or_imprecise_dtypes=True))
+
+    k_f0 = inc(v.memset(tab[:, 0:1024], 8.0))
+    W("s", k_f0)
+    k_f1 = inc(s.activation(tab[:, 1024:2048], tab[:, 0:1024], AF.Copy))
+    W("s", k_f1)
+    inc(s.activation(tab[:, 2048:4096], tab[:, 0:2048], AF.Copy), k_fill)
+
+    k_z = inc(v.memset(T["zz"][:], 0.0))
+    W("v", k_i)
+    k1 = inc(v.tensor_scalar(T["pb"][:], T["ip"][:, 0:1], 1, None, OP.bitwise_and))
+    W("v", k1)
+    k2 = inc(v.tensor_copy(T["ml"][:], T["pb"][:]))
+    k3 = inc(v.tensor_scalar(T["nml"][:], T["pb"][:], -1.0, 1.0, OP.mult, OP.add))
+    W("v", k3)
+    inc(v.tensor_scalar(T["hb"][:], T["io8"][:], T["nml"][:, 0:1], None, OP.mult), k2)
+    W("v", k2, k_lo)
+    k_vr = tok()
+    for b in range(8):
+        inc(v.tensor_scalar(T["vr"][:, 256 * b:256 * b + 256], T["lo"][:], T["ml"][:, 0:1], T["hb"][:, b:b + 1], OP.mult, OP.add), k_vr)
+    W("v", l_nx)
+    k_n16 = inc(v.tensor_copy(T["nxt16"][:], T["nxi"][:]))
+    inc(v.memset(tab[:, 4096:8192 - GF], 8.0), k_fill)
+    W("v", l_ow)
+    k_o16 = inc(v.tensor_copy(T["own16"][:], T["owi"][:]))
+    W("v", l_pt)
+    k_p0 = inc(v.tensor_copy(T["pt0"][:], T["pti"][:]))
+    W("v", k_f0, k_f1, k_fill, k_vr, k_o16)
+    k_tab = inc(v.tensor_copy(tab[:, 0:8192].indirect(T["own16"][:, 0:128]), T["vr"][:]))
+
+    A, B = helpers(T, topo, core)
+    sent = 0
+    W("g", k_n16)
+    sent += write(g, T, topo, core, A, T["rln"][:], T["nxt16"][:], "rn")
+    W("g", k_z)
+    kb = inc(g.affine_select(T["basef"][:], T["zz"][:, 0:144], [[-512, 9], [1, 16]], OP.not_equal, 256.0, -15, 32))
+    k_ids = inc(g.affine_select(T["ids"][:], T["zz"][:], [[1, 160]], OP.not_equal, 1.0, -16, -1))
+    W("g", kb)
+    k_bf = inc(g.affine_select(T["basef"][:], T["basef"][:], [[-512, 9], [1, 16]], OP.not_equal, 1.0, -47, 32))
+    W("g", k_p0)
+    sent += write(g, T, topo, core, B, T["rlp"][:], T["pt0"][:], "rp")
+    sent += writes(g, T, topo, core, [(T.cores[(q - 4) % N], T["pt4"][:], T["pt0"][:], "ap4", 0, 4),
+                                      (T.cores[(q - 2) % N], T["pt2"][:], T["pt0"][:], "ap2", 4, 8)])
+
+    def gather2(outb, win, lst):
+        ks = []
+        for h in range(2):
+            k = tok()
+            a = 1024 * h
+            inc(v.tensor_copy(outb[:, a:a + 512], win.indirect(lst[:, a // 16:a // 16 + 32])), k)
+            inc(s.activation(outb[:, a + 512:a + 1024], win.indirect(lst[:, a // 16 + 32:a // 16 + 64]), AF.Copy), k)
+            ks.append(k)
+        return ks
+
+    R("v", "anx", 8)
+    R("s", "anx", 8)
+    W("v", k_tab)
+    W("s", k_tab)
+    kg = gather2(T["gr"], tab[:, 0:8192], T["nx"])
+
+    psa = T["psa"]
+    freed = [None] * 4
+
+    def row_mm(kk):
+        ks = []
+        for b in range(4):
+            if freed[b]:
+                W("t", freed[b])
+            k = tok()
+            for p in range(4 * b, 4 * b + 4):
+                o = 16 + p - kk
+                inc(t.matmul(psa[:, 128 * p:128 * p + 128], T["ids"][:, o:o + 128], T["pt%d" % kk][:], True, True), k)
+            ks.append(k)
+        return ks
+
+    def row_copy(kk, eng, out, ks):
+        done = tok()
+        for b in range(4):
+            W(eng, ks[b])
+            c = slice(512 * b, 512 * b + 512)
+            f = tok() if kk else done
+            if eng == "v":
+                inc(v.tensor_scalar(out[:, c], psa[:, c], T["mk"][:, kk:kk + 1], None, OP.mult), f)
+            else:
+                inc(s.activation(out[:, c], psa[:, c], AF.Identity, scale=T["mk"][:, kk:kk + 1]), f)
+            freed[b] = f
+        return done if not kk else list(freed)
+
+    W("t", k_ids)
+    R("t", "ap5", AP_ENG[5])
+    m5 = row_mm(5)
+
+    W("t", k_bf)
+    kw = []
+    for h, pw in ((0, T["pwa"]), (1, T["pwb"])):
+        W("t", kg[h])
+        for p in range(16):
+            op = t.matmul(pw[:, 0:64], T["basef"][:, 15 - p:143 - p], T["gr"][:, 1024 * h + p:1024 * h + 1024:16], p == 0, p == 15)
+        kw.append(inc(op))
+
+    k1 = inc(v.tensor_scalar(T["ps"][:], T["ip"][:, 0:1], 15, None, OP.bitwise_and))
+    W("v", k1)
+    k2 = inc(v.tensor_copy(T["sf"][:], T["ps"][:]))
+    W("v", k2)
+    k_mk = inc(v.tensor_scalar(T["mk"][:], T["io8"][:], T["sf"][:, 0:1], None, OP.is_equal))
+    k_f = tok()
+    for h, pw in ((0, T["pwa"]), (1, T["pwb"])):
+        W("v", kw[h])
+        inc(v.tensor_copy(T["f0"][:, 64 * h:64 * h + 64], pw[:, 0:64]), k_f)
+
+    W("g", k_f)
+    sent += write(g, T, topo, core, A, T["rlf"][:], T["f0"][:], "rf")
+    sent += writes(g, T, topo, core, [(T.cores[(q - 4) % N], T["f4"][:], T["f0"][:], "af4", 0, 4),
+                                      (T.cores[(q - 2) % N], T["f2"][:], T["f0"][:], "af2", 4, 8)])
+    W("s", k_mk)
+    w5 = row_copy(5, "s", T["wa"], m5)
+    R("t", "ap4", AP_ENG[4])
+    m4 = row_mm(4)
+    W("v", k_mk)
+    w4 = row_copy(4, "v", T["pr4"], m4)
+    rows = {4: w4}
+    for kk in (3, 2, 1, 0):
+        if kk:
+            R("t", "ap%d" % kk, AP_ENG[kk])
+        else:
+            W("t", k_p0)
+        mm = row_mm(kk)
+        rows[kk] = row_copy(kk, "s", T["pr%d" % kk], mm)
+
+    k_c = inc(v.memset(T["wa"][:, 2048:2064], -2048.0))
+    inc(v.memset(T["wb"][:, 2048:2064], -2048.0), k_c)
+    k_on = inc(v.memset(T["on"][:], 1.0))
+    inc(v.memset(T["half"][:], 0.5), k_c)
+    for b in ("sumw", "posk", "nlo", "nhi"):
+        inc(v.memset(T[b][:, 128:144], 0.0), k_c)
+    inc(v.memset(T["sc1"][:, 0:16], 0.0), k_c)
+    k1 = inc(v.tensor_scalar(T["pg"][:], T["ip"][:, 0:1], 4, 1, OP.arith_shift_right, OP.bitwise_and))
+    k3 = inc(v.tensor_scalar(T["loi"][:], T["owi"][:], 255, None, OP.bitwise_and))
+    W("v", k1, k_on)
+    k2 = inc(v.tensor_copy(T["gf"][:], T["pg"][:]))
+    inc(v.tensor_scalar(T["ngf"][:], T["pg"][:], -1.0, 1.0, OP.mult, OP.add), k2)
+    W("v", k3)
+    inc(v.tensor_scalar(T["nlo"][:, 0:128], T["loi"][:], 1.0, None, OP.add), k_c)
+    inc(v.tensor_tensor(T["nhi"][:, 0:128], T["owi"][:], T["loi"][:], OP.subtract), k_c)
+    W("v", k2)
+    inc(v.tensor_scalar(T["msk"][:, 0:16], T["on"][:, 0:16], T["ngf"][:, 0:1], None, OP.mult), k_c)
+    inc(v.tensor_scalar(T["msk"][:, 16:32], T["on"][:, 0:16], T["gf"][:, 0:1], None, OP.mult), k_c)
+
+    W("g", k_on)
+    k1 = inc(g.affine_select(T["bases"][:], T["on"][:, 0:144], [[0, 9], [1, 16]], OP.is_equal, 0.0, -15, 0))
+    inc(g.affine_select(T["bo"][:], T["on"][:, 0:128], [[-16, 8], [0, 16]], OP.is_ge, 0.0, 0, 1), k1)
+    k_kc = inc(g.iota(T["kc"][:], [[0, 8], [1, 16]], 0, 0, allow_small_or_imprecise_dtypes=True))
+    inc(g.iota(T["m1"][:], [[1, 256]], 1, 0, allow_small_or_imprecise_dtypes=True), k_kc)
+    W("g", k1)
+    k2 = inc(g.affine_select(T["bases"][:], T["bases"][:], [[-16, 9], [0, 16]], OP.is_ge, 0.0, 0, 1))
+    inc(g.affine_select(T["bo"][:], T["bo"][:], [[16, 8], [0, 16]], OP.is_ge, 0.0, 15, -1), k2)
+    W("g", k2)
+    k_b = inc(g.affine_select(T["bases"][:], T["bases"][:], [[16, 9], [0, 16]], OP.is_ge, 0.0, 5, -1))
+    inc(g.affine_select(T["tri"][:], T["bo"][:], [[1, 128]], OP.is_ge, 0.0, 0, -1), k_b)
+
+    W("s", k_kc, k2)
+    k_sc = inc(s.activation(T["cp"][:], T["kc"][:], AF.Copy, scale=-1.0 / 2048))
+    inc(s.activation(T["ck"][:], T["kc"][:], AF.Copy, scale=-1.0 / 128), k_sc)
+    inc(s.activation(T["bo16"][:], T["bo"][:], AF.Copy, scale=1.0 / 16), k_sc)
+    inc(s.activation(T["bo32"][:], T["bo"][:, 0:128:16], AF.Copy), k_sc)
+
+    wa, wb = T["wa"], T["wb"]
+    W("v", k_c, *w5)
+    src, dst, kd = wa, wb, None
+    for kk in (4, 3, 2, 1):
+        R("v", "af%d" % (kk + 1), AF_ENG[kk + 1])
+        W("v", *rows[kk])
+        if kd:
+            W("v", kd)
+        kd = inc(v.tensor_tensor(dst[:, 0:2048], src[:, 0:2064].indirect(T["f%d" % (kk + 1)][:]), T["pr%d" % kk][:], OP.add))
+        src, dst = dst, src
+
+    W("t", k_b, rows[0], k_f)
+    pws = (T["pwa"], T["pwb"])
+    for h in range(2):
+        for p in range(16):
+            t.matmul(pws[h][:, 0:64], T["bases"][:, 15 - p:143 - p], T["pr0"][:, 1024 * h + p:1024 * h + 1024:16], p == 0, False)
+    T1, T2, T3, CM = psa[:, 0:128], psa[:, 512:640], psa[:, 1024:1152], psa[:, 1536:1568]
+    W("t", k_sc, k_kc, k_on)
+    t.matmul(T3, T["on"][:, 0:128], T["ck"][:], True, False)
+    t.matmul(T2, T["on"][:, 0:128], T["cp"][:], True, False)
+
+    R("v", "af1", AF_ENG[1])
+    R("s", "af1", AF_ENG[1])
+    W("v", kd)
+    W("s", kd)
+    kr = gather2(T["rr"], src[:, 0:2064], T["f1"])
+    kw = []
+    for h in range(2):
+        W("t", kr[h])
+        for p in range(16):
+            op = t.matmul(pws[h][:, 0:64], T["bases"][:, 15 - p:143 - p], T["rr"][:, 1024 * h + p:1024 * h + 1024:16], False, p == 15)
+        kw.append(inc(op))
+
+    kt, sc1 = T["kt"], T["sc1"]
+    kk_ = []
+    for h in range(2):
+        W("v", kw[h])
+        kk_.append(inc(v.tensor_scalar(kt[:, 64 * h:64 * h + 64], pws[h][:, 0:64], 0.0, None, OP.is_ge)))
+    W("v", *kk_)
+    k_scan = inc(v.tensor_tensor_scan(sc1[:, 16:144], kt[:], kt[:], 0.0, OP.add, OP.max))
+    k_sum = tok()
+    for h in range(2):
+        W("s", kk_[h])
+        inc(s.activation(T["sumw"][:, 64 * h:64 * h + 64], pws[h][:, 0:64], AF.Copy), k_sum)
+    W("t", k_scan, k_c)
+    k_t1 = inc(t.matmul(T1, sc1[:, 16:144], T["bo16"][:], True, True))
+    k_t3 = inc(t.matmul(T3, sc1[:, 16:144], T["bo16"][:], False, True))
+    k_t2 = inc(t.matmul(T2, sc1[:, 16:144], T["bo16"][:], False, True))
+    t.matmul(T["px"][:, 0:128], T["bo"][:], sc1[:, 15:143], True, False)
+    k_pos = inc(t.matmul(T["px"][:, 0:128], T["tri"][:], kt[:], False, True))
+    W("v", k_t1)
+    k_a = inc(v.tensor_scalar(T["ai"][:], T1, -0.46875, None, OP.add))
+    W("s", k_t3)
+    k_sg = inc(s.activation(T["sg"][:], T3, AF.Sign, bias=-0.03125, scale=-1.0))
+    W("v", k_a, k_t2)
+    k_ab = inc(v.tensor_tensor(T["a1"][:], T2, T["ai"][:], OP.is_le))
+    W("v", k_kc)
+    inc(v.tensor_tensor(T["bb"][:], T["ai"][:], T["kc"][:], OP.is_equal), k_ab)
+    W("t", k_sg, k_ab)
+    for a in range(4):
+        c = slice(32 * a, 32 * a + 32)
+        t.matmul(psa[c, 1536:1568], T["half"][:], T["sg"][:, c], True, False)
+        op = t.matmul(psa[c, 1536:1568], T["a1"][:, c], T["bb"][:, c], False, True)
+        k_cm = inc(op, None if a == 0 else k_cm)
+    W("v", k_pos)
+    k_pk = inc(v.tensor_tensor(T["posk"][:, 0:128], T["px"][:, 0:128], kt[:], OP.mult))
+    W("v", k_cm)
+    k1 = inc(v.tensor_tensor(T["cmm"][:], CM, T["msk"][:], OP.mult))
+    W("v", k1)
+    k2 = inc(v.tensor_tensor(T["lf"][:], T["cmm"][:, 0:16], T["cmm"][:, 16:32], OP.add))
+    W("v", k2)
+    k3 = inc(v.tensor_scalar(T["lst"][:], T["lf"][:], 64.0, None, OP.add))
+    W("v", k3, k_pk)
+    k_oh = inc(v.tensor_tensor(T["oh"][:], T["posk"][:].indirect(T["lst"][:]), T["m1"][:], OP.is_equal))
+    W("v", k_oh, k_sum)
+    k_vs = inc(v.tensor_tensor(T["vs"][:], T["sumw"][:].indirect(T["lst"][:]), T["oh"][:], OP.mult))
+    k_vh = inc(v.tensor_tensor(T["vh"][:], T["nhi"][:].indirect(T["lst"][:]), T["oh"][:], OP.mult))
+    k_vl = inc(v.tensor_tensor(T["vl"][:], T["nlo"][:].indirect(T["lst"][:]), T["oh"][:], OP.mult))
+    W("t", k_vs)
+    k_ys = inc(t.matmul(T["px"][0:8, 0:256], T["bo32"][:], T["vs"][:], True, True))
+    W("t", k_vh)
+    t.matmul(T["py"][0:8, 0:256], T["bo"][:, 0:128:16], T["vh"][:], True, False)
+    W("t", k_vl)
+    k_yk = inc(t.matmul(T["py"][0:8, 0:256], T["bo"][:, 0:128:16], T["vl"][:], False, True))
+    W("s", k_ys)
+    k1 = inc(s.activation(T["yss"][0:8, :], T["px"][0:8, 0:256], AF.Copy))
+    W("s", k1)
+    o1 = inc(g.scalar.dma_start(T.ys[:], T["yss"][0:8, :]), None, 16)
+    W("v", k_yk)
+    k2 = inc(v.tensor_scalar(T["yks"][0:8, :], T["py"][0:8, 0:256], -1.0, None, OP.add))
+    W("y", k2)
+    o2 = inc(g.sync.dma_start(T.yk[:], T["yks"][0:8, :]), None, 16)
+    W("s", o1)
+    W("y", o2)
+    g.wait_ge(T.sem["lc"], sent)

@@ -7,8 +7,11 @@ SCRATCH = {
     "owi": ("sbuf", [128, 128], "int32"), "nxi": ("sbuf", [128, 128], "int32"), "pti": ("sbuf", [128, 128], "int32"),
     "own16": ("sbuf", [128, 128], "uint16"), "nxt16": ("sbuf", [128, 128], "uint16"), "pt0": ("sbuf", [128, 128], "bfloat16"),
     "tab": ("sbuf", [128, 8192], "bfloat16"), "vr": ("sbuf", [128, 2048], "bfloat16"), "gr": ("sbuf", [128, 2048], "bfloat16"),
-    "f0": ("sbuf", [128, 128], "uint16"),
-    "wa": ("sbuf", [128, 2064], "bfloat16"), "wb": ("sbuf", [128, 2064], "bfloat16"), "rr": ("sbuf", [128, 2048], "bfloat16"),
+    "f0": ("sbuf", [128, 128], "uint16"), "fg": ("sbuf", [128, 128], "uint16"),
+    "xs": ("dram", [128, 256], "bfloat16"), "xr": ("dram", [128, 256], "bfloat16"),
+    "xw": ("sbuf", [128, 2064], "bfloat16"), "xg": ("sbuf", [128, 2048], "bfloat16"),
+    "wa": ("sbuf", [128, 2064], "bfloat16"), "wb": ("sbuf", [128, 2064], "bfloat16"), "w4": ("sbuf", [128, 2064], "bfloat16"),
+    "b3": ("sbuf", [128, 2048], "bfloat16"), "rr": ("sbuf", [128, 2048], "bfloat16"),
     "lo": ("sbuf", [128, 256], "bfloat16"), "m1": ("sbuf", [128, 256], "bfloat16"), "ip": ("sbuf", [128, 2], "int32"),
     "io8": ("sbuf", [128, 8], "float32"), "pb": ("sbuf", [128, 1], "int32"), "ps": ("sbuf", [128, 1], "int32"),
     "pg": ("sbuf", [128, 1], "int32"),
@@ -31,15 +34,16 @@ SCRATCH = {
     "px": ("psum", [128, 512], "float32"), "py": ("psum", [128, 512], "float32"),
 }
 for _k in range(1, 6):
-    SCRATCH["f%d" % _k] = ("sbuf", [128, 128], "uint16")
+    if _k != 2:
+        SCRATCH["f%d" % _k] = ("sbuf", [128, 128], "uint16")
     SCRATCH["pt%d" % _k] = ("sbuf", [128, 128], "bfloat16")
-for _k in range(5):
+for _k in (0, 2, 3):
     SCRATCH["pr%d" % _k] = ("sbuf", [128, 2048], "bfloat16")
 NTOK = 126
-SEMAPHORES = (["t%d" % _k for _k in range(NTOK)] + ["anx", "rn", "rf", "rp", "lc"]
-              + ["af%d" % _k for _k in range(1, 6)] + ["ap%d" % _k for _k in range(1, 6)])
+SEMAPHORES = (["t%d" % _k for _k in range(NTOK)] + ["anx", "rn", "rf", "rp", "lc", "ax", "af1", "af3", "af4", "af5"]
+              + ["ap%d" % _k for _k in range(1, 6)])
 
-ODD, EVEN = (5, 3, 1), (4, 2)
+ODD = (5, 3, 1)
 
 
 def engs(topo, src, dst, a, b):
@@ -96,7 +100,7 @@ def hand_on(g, core, T, topo):
             g.wait_ge(T.sem["lc"], sent)
 
 
-AF_ENG = {5: 8, 4: 4, 3: 4, 2: 4, 1: 4}
+AF_ENG = {5: 8, 4: 8, 3: 4, 1: 4}
 AP_ENG = {5: 4, 4: 4, 3: 2, 2: 4, 1: 2}
 
 
@@ -109,6 +113,7 @@ def rank_program(g, core, T, topo):
     Q = {"g": g, "v": g.vector, "s": g.scalar, "t": g.tensor, "y": g.sync}
     v, s, t = g.vector, g.scalar, g.tensor
     used, seen = [0], {}
+    small = {"allow_small_or_imprecise_dtypes": True}
 
     def tok():
         used[0] += 1
@@ -137,10 +142,10 @@ def rank_program(g, core, T, topo):
 
     tab = T["tab"]
     k_i = inc(g.iota(T["ip"][:, 0:1], [[0, 1]], 0, 1))
-    inc(g.iota(T["io8"][:], [[1, 8]], 0, 0, allow_small_or_imprecise_dtypes=True), k_i)
-    k_lo = inc(g.iota(T["lo"][:], [[1, 256]], 0, 0, allow_small_or_imprecise_dtypes=True))
+    inc(g.iota(T["io8"][:], [[1, 8]], 0, 0, **small), k_i)
+    k_lo = inc(g.iota(T["lo"][:], [[1, 256]], 0, 0, **small))
     GF = 768
-    k_fill = inc(g.iota(tab[:, 8192 - GF:8192], [[0, GF]], 8, 0, allow_small_or_imprecise_dtypes=True))
+    k_fill = inc(g.iota(tab[:, 8192 - GF:8192], [[0, GF]], 8, 0, **small))
 
     k_f0 = inc(v.memset(tab[:, 0:1024], 8.0))
     W("s", k_f0)
@@ -169,6 +174,9 @@ def rank_program(g, core, T, topo):
     k_p0 = inc(v.tensor_copy(T["pt0"][:], T["pti"][:]))
     W("v", k_f0, k_f1, k_fill, k_vr, k_o16)
     k_tab = inc(v.tensor_copy(tab[:, 0:8192].indirect(T["own16"][:, 0:128]), T["vr"][:]))
+    W("s", k_vr)
+    k_sz = inc(s.activation(T["xw"][:, 0:2048], T["vr"][:], AF.Copy, scale=0.0))
+    inc(s.activation(T["pr2"][:], T["vr"][:], AF.Copy, scale=0.0), k_sz)
 
     A, B = helpers(T, topo, core)
     sent = 0
@@ -183,6 +191,11 @@ def rank_program(g, core, T, topo):
     sent += write(g, T, topo, core, B, T["rlp"][:], T["pt0"][:], "rp")
     sent += writes(g, T, topo, core, [(T.cores[(q - 4) % N], T["pt4"][:], T["pt0"][:], "ap4", 0, 4),
                                       (T.cores[(q - 2) % N], T["pt2"][:], T["pt0"][:], "ap2", 4, 8)])
+    k_on = inc(g.iota(T["on"][:], [[0, 160]], 1, 0, **small))
+    k_c = tok()
+    for name, a, val in (("wa", 2048, -2048), ("wb", 2048, -2048), ("w4", 2048, 0), ("xw", 2048, 8),
+                         ("sumw", 128, 0), ("posk", 128, 0), ("nlo", 128, 0), ("nhi", 128, 0), ("sc1", 0, 0)):
+        inc(g.iota(T[name][:, a:a + 16], [[0, 16]], val, 0, **small), k_c)
 
     def gather2(outb, win, lst):
         ks = []
@@ -210,27 +223,25 @@ def rank_program(g, core, T, topo):
                 W("t", freed[b])
             k = tok()
             for p in range(4 * b, 4 * b + 4):
-                o = 16 + p - kk
+                o = 14 + p - kk
                 inc(t.matmul(psa[:, 128 * p:128 * p + 128], T["ids"][:, o:o + 128], T["pt%d" % kk][:], True, True), k)
             ks.append(k)
         return ks
 
     def row_copy(kk, eng, out, ks):
-        done = tok()
         for b in range(4):
             W(eng, ks[b])
             c = slice(512 * b, 512 * b + 512)
-            f = tok() if kk else done
             if eng == "v":
-                inc(v.tensor_scalar(out[:, c], psa[:, c], T["mk"][:, kk:kk + 1], None, OP.mult), f)
+                op = v.tensor_scalar(out[:, c], psa[:, c], T["mk"][:, 2 + kk:3 + kk], None, OP.mult)
             else:
-                inc(s.activation(out[:, c], psa[:, c], AF.Identity, scale=T["mk"][:, kk:kk + 1]), f)
-            freed[b] = f
-        return done if not kk else list(freed)
+                op = s.activation(out[:, c], psa[:, c], AF.Identity, scale=T["mk"][:, 2 + kk:3 + kk])
+            freed[b] = inc(op)
+        return list(freed)
 
     W("t", k_ids)
-    R("t", "ap5", AP_ENG[5])
-    m5 = row_mm(5)
+    R("t", "ap4", AP_ENG[4])
+    m4 = row_mm(4)
 
     W("t", k_bf)
     kw = []
@@ -241,10 +252,17 @@ def rank_program(g, core, T, topo):
         kw.append(inc(op))
 
     k1 = inc(v.tensor_scalar(T["ps"][:], T["ip"][:, 0:1], 15, None, OP.bitwise_and))
+    k3 = inc(v.tensor_scalar(T["pg"][:], T["ip"][:, 0:1], 4, 1, OP.arith_shift_right, OP.bitwise_and))
     W("v", k1)
     k2 = inc(v.tensor_copy(T["sf"][:], T["ps"][:]))
     W("v", k2)
     k_mk = inc(v.tensor_scalar(T["mk"][:], T["io8"][:], T["sf"][:, 0:1], None, OP.is_equal))
+    W("v", k3)
+    k2 = inc(v.tensor_copy(T["gf"][:], T["pg"][:]))
+    inc(v.tensor_scalar(T["ngf"][:], T["pg"][:], -1.0, 1.0, OP.mult, OP.add), k2)
+    W("v", k2, k_on)
+    k_nm = inc(v.tensor_scalar(T["msk"][:, 0:16], T["on"][:, 0:16], T["ngf"][:, 0:1], None, OP.mult))
+    inc(v.tensor_scalar(T["msk"][:, 16:32], T["on"][:, 0:16], T["gf"][:, 0:1], None, OP.mult), k_nm)
     k_f = tok()
     for h, pw in ((0, T["pwa"]), (1, T["pwb"])):
         W("v", kw[h])
@@ -252,86 +270,103 @@ def rank_program(g, core, T, topo):
 
     W("g", k_f)
     sent += write(g, T, topo, core, A, T["rlf"][:], T["f0"][:], "rf")
-    sent += writes(g, T, topo, core, [(T.cores[(q - 4) % N], T["f4"][:], T["f0"][:], "af4", 0, 4),
-                                      (T.cores[(q - 2) % N], T["f2"][:], T["f0"][:], "af2", 4, 8)])
+    sent += write(g, T, topo, core, T.cores[(q - 4) % N], T["f4"][:], T["f0"][:], "af4")
+    W("y", *kg)
+    k_xs = inc(g.sync.dma_start(T["xs"][0:64, :], T["gr"][0:128:16, :]), None, 16)
+    inc(g.sync.dma_start(T["xs"][64:128, :], T["gr"][1:128:16, :]), k_xs, 16)
+    W("g", k_xs)
+    sent += write(g, T, topo, core, T.cores[(q - 2) % N], T["xr"][:], T["xs"][:], "ax")
+    k_z0 = inc(g.iota(T["pr0"][:], [[0, 2048]], 0, 0, **small))
+    W("y", k_sz)
+    R("y", "ap2", AP_ENG[2])
+    k_r2 = inc(g.sync.dma_start(T["pr2"][4:128:16, :], T["pt2"][:]), None, 16)
+    R("y", "ap1", AP_ENG[1])
+    k_xw = inc(g.sync.dma_start(T["xw"][3:128:16, 0:2048], T["pt1"][:]), None, 16)
+    R("y", "ax", 8)
+    inc(g.sync.dma_start(T["xw"][0:128:16, 0:2048], T["xr"][0:64, :]), k_xw, 16)
+    inc(g.sync.dma_start(T["xw"][1:128:16, 0:2048], T["xr"][64:128, :]), k_xw, 16)
+    W("y", k_z0, k_p0)
+    k_r0 = inc(g.sync.dma_start(T["pr0"][2:128:16, :], T["pt0"][:]), None, 16)
+
     W("s", k_mk)
+    w4 = row_copy(4, "s", T["w4"], m4)
+    R("t", "ap3", AP_ENG[3])
+    m3 = row_mm(3)
+    w3 = row_copy(3, "v", T["pr3"], m3)
+    R("t", "ap5", AP_ENG[5])
+    m5 = row_mm(5)
     w5 = row_copy(5, "s", T["wa"], m5)
-    R("t", "ap4", AP_ENG[4])
-    m4 = row_mm(4)
-    W("v", k_mk)
-    w4 = row_copy(4, "v", T["pr4"], m4)
-    rows = {4: w4}
-    for kk in (3, 2, 1, 0):
-        if kk:
-            R("t", "ap%d" % kk, AP_ENG[kk])
-        else:
-            W("t", k_p0)
-        mm = row_mm(kk)
-        rows[kk] = row_copy(kk, "s", T["pr%d" % kk], mm)
 
-    k_c = inc(v.memset(T["wa"][:, 2048:2064], -2048.0))
-    inc(v.memset(T["wb"][:, 2048:2064], -2048.0), k_c)
-    k_on = inc(v.memset(T["on"][:], 1.0))
-    inc(v.memset(T["half"][:], 0.5), k_c)
-    for b in ("sumw", "posk", "nlo", "nhi"):
-        inc(v.memset(T[b][:, 128:144], 0.0), k_c)
-    inc(v.memset(T["sc1"][:, 0:16], 0.0), k_c)
-    k1 = inc(v.tensor_scalar(T["pg"][:], T["ip"][:, 0:1], 4, 1, OP.arith_shift_right, OP.bitwise_and))
     k3 = inc(v.tensor_scalar(T["loi"][:], T["owi"][:], 255, None, OP.bitwise_and))
-    W("v", k1, k_on)
-    k2 = inc(v.tensor_copy(T["gf"][:], T["pg"][:]))
-    inc(v.tensor_scalar(T["ngf"][:], T["pg"][:], -1.0, 1.0, OP.mult, OP.add), k2)
     W("v", k3)
-    inc(v.tensor_scalar(T["nlo"][:, 0:128], T["loi"][:], 1.0, None, OP.add), k_c)
-    inc(v.tensor_tensor(T["nhi"][:, 0:128], T["owi"][:], T["loi"][:], OP.subtract), k_c)
-    W("v", k2)
-    inc(v.tensor_scalar(T["msk"][:, 0:16], T["on"][:, 0:16], T["ngf"][:, 0:1], None, OP.mult), k_c)
-    inc(v.tensor_scalar(T["msk"][:, 16:32], T["on"][:, 0:16], T["gf"][:, 0:1], None, OP.mult), k_c)
+    inc(v.tensor_scalar(T["nlo"][:, 0:128], T["loi"][:], 1.0, None, OP.add), k_nm)
+    inc(v.tensor_tensor(T["nhi"][:, 0:128], T["owi"][:], T["loi"][:], OP.subtract), k_nm)
 
-    W("g", k_on)
     k1 = inc(g.affine_select(T["bases"][:], T["on"][:, 0:144], [[0, 9], [1, 16]], OP.is_equal, 0.0, -15, 0))
     inc(g.affine_select(T["bo"][:], T["on"][:, 0:128], [[-16, 8], [0, 16]], OP.is_ge, 0.0, 0, 1), k1)
-    k_kc = inc(g.iota(T["kc"][:], [[0, 8], [1, 16]], 0, 0, allow_small_or_imprecise_dtypes=True))
-    inc(g.iota(T["m1"][:], [[1, 256]], 1, 0, allow_small_or_imprecise_dtypes=True), k_kc)
+    k_kc = inc(g.iota(T["kc"][:], [[0, 8], [1, 16]], 0, 0, **small))
+    inc(g.iota(T["m1"][:], [[1, 256]], 1, 0, **small), k_kc)
     W("g", k1)
-    k2 = inc(g.affine_select(T["bases"][:], T["bases"][:], [[-16, 9], [0, 16]], OP.is_ge, 0.0, 0, 1))
+    k2 = inc(g.affine_select(T["bases"][:], T["bases"][:], [[-16, 9], [0, 16]], OP.is_ge, 0.0, -2, 1))
     inc(g.affine_select(T["bo"][:], T["bo"][:], [[16, 8], [0, 16]], OP.is_ge, 0.0, 15, -1), k2)
     W("g", k2)
-    k_b = inc(g.affine_select(T["bases"][:], T["bases"][:], [[16, 9], [0, 16]], OP.is_ge, 0.0, 5, -1))
+    k_b = inc(g.affine_select(T["bases"][:], T["bases"][:], [[16, 9], [0, 16]], OP.is_ge, 0.0, 7, -1))
     inc(g.affine_select(T["tri"][:], T["bo"][:], [[1, 128]], OP.is_ge, 0.0, 0, -1), k_b)
+
+    wa, wb = T["wa"], T["wb"]
+    R("v", "af4", AF_ENG[4])
+    W("v", k_c, *w4)
+    W("v", *w3)
+    k_b3 = inc(v.tensor_tensor(T["b3"][:], T["w4"][:].indirect(T["f4"][:]), T["pr3"][:], OP.add))
+    SP = 1280
+    R("s", "af5", AF_ENG[5])
+    W("s", k_c, *w5)
+    k_d1 = inc(s.activation(wb[:, 0:SP], wa[:].indirect(T["f5"][:, 0:SP // 16]), AF.Copy))
+    R("v", "af5", AF_ENG[5])
+    W("v", *w5)
+    inc(v.tensor_copy(wb[:, SP:2048], wa[:].indirect(T["f5"][:, SP // 16:128])), k_d1)
+    W("v", k_d1, k_b3)
+    k_d2 = inc(v.tensor_tensor(wa[:, 0:2048], wb[:].indirect(T["f4"][:]), T["b3"][:], OP.add))
+    R("v", "af3", AF_ENG[3])
+    W("v", k_d2, k_r2)
+    k_d3 = inc(v.tensor_tensor(wb[:, 0:2048], wa[:].indirect(T["f3"][:]), T["pr2"][:], OP.add))
+
+    R("s", "af1", AF_ENG[1])
+    W("s", k_xw)
+    pws = (T["pwa"], T["pwb"])
+    pqs = (T["px"], T["py"])
+    kq, k_xg, k_fg = [], [], tok()
+    for h in range(2):
+        k_xg.append(inc(s.activation(T["xg"][:, 1024 * h:1024 * h + 1024],
+                                     T["xw"][:].indirect(T["f1"][:, 64 * h:64 * h + 64]), AF.Copy)))
+        W("t", k_xg[h])
+        for p in range(16):
+            op = t.matmul(pqs[h][:, 0:64], T["basef"][:, 15 - p:143 - p], T["xg"][:, 1024 * h + p:1024 * h + 1024:16], p == 0, p == 15)
+        kq.append(inc(op))
+    for h in range(2):
+        W("v", kq[h])
+        inc(v.tensor_copy(T["fg"][:, 64 * h:64 * h + 64], pqs[h][:, 0:64]), k_fg)
 
     W("s", k_kc, k2)
     k_sc = inc(s.activation(T["cp"][:], T["kc"][:], AF.Copy, scale=-1.0 / 2048))
     inc(s.activation(T["ck"][:], T["kc"][:], AF.Copy, scale=-1.0 / 128), k_sc)
     inc(s.activation(T["bo16"][:], T["bo"][:], AF.Copy, scale=1.0 / 16), k_sc)
     inc(s.activation(T["bo32"][:], T["bo"][:, 0:128:16], AF.Copy), k_sc)
+    inc(s.activation(T["half"][:], T["on"][:, 0:32], AF.Copy, scale=0.5), k_sc)
 
-    wa, wb = T["wa"], T["wb"]
-    W("v", k_c, *w5)
-    src, dst, kd = wa, wb, None
-    for kk in (4, 3, 2, 1):
-        R("v", "af%d" % (kk + 1), AF_ENG[kk + 1])
-        W("v", *rows[kk])
-        if kd:
-            W("v", kd)
-        kd = inc(v.tensor_tensor(dst[:, 0:2048], src[:, 0:2064].indirect(T["f%d" % (kk + 1)][:]), T["pr%d" % kk][:], OP.add))
-        src, dst = dst, src
-
-    W("t", k_b, rows[0], k_f)
-    pws = (T["pwa"], T["pwb"])
-    for h in range(2):
-        for p in range(16):
-            t.matmul(pws[h][:, 0:64], T["bases"][:, 15 - p:143 - p], T["pr0"][:, 1024 * h + p:1024 * h + 1024:16], p == 0, False)
+    W("t", k_b, k_f, k_r0)
+    for b in ("xg", "pr0"):
+        for h in range(2):
+            for p in range(16):
+                t.matmul(pws[h][:, 0:64], T["bases"][:, 15 - p:143 - p], T[b][:, 1024 * h + p:1024 * h + 1024:16], b == "xg" and p == 0, False)
     T1, T2, T3, CM = psa[:, 0:128], psa[:, 512:640], psa[:, 1024:1152], psa[:, 1536:1568]
-    W("t", k_sc, k_kc, k_on)
+    W("t", k_sc, *w5)
     t.matmul(T3, T["on"][:, 0:128], T["ck"][:], True, False)
     t.matmul(T2, T["on"][:, 0:128], T["cp"][:], True, False)
 
-    R("v", "af1", AF_ENG[1])
-    R("s", "af1", AF_ENG[1])
-    W("v", kd)
-    W("s", kd)
-    kr = gather2(T["rr"], src[:, 0:2064], T["f1"])
+    W("v", k_d3, k_fg)
+    W("s", k_d3, k_fg)
+    kr = gather2(T["rr"], wb[:], T["fg"])
     kw = []
     for h in range(2):
         W("t", kr[h])
@@ -350,7 +385,7 @@ def rank_program(g, core, T, topo):
     for h in range(2):
         W("s", kk_[h])
         inc(s.activation(T["sumw"][:, 64 * h:64 * h + 64], pws[h][:, 0:64], AF.Copy), k_sum)
-    W("t", k_scan, k_c)
+    W("t", k_scan, k_c, k_fg)
     k_t1 = inc(t.matmul(T1, sc1[:, 16:144], T["bo16"][:], True, True))
     k_t3 = inc(t.matmul(T3, sc1[:, 16:144], T["bo16"][:], False, True))
     k_t2 = inc(t.matmul(T2, sc1[:, 16:144], T["bo16"][:], False, True))
@@ -372,7 +407,7 @@ def rank_program(g, core, T, topo):
         k_cm = inc(op, None if a == 0 else k_cm)
     W("v", k_pos)
     k_pk = inc(v.tensor_tensor(T["posk"][:, 0:128], T["px"][:, 0:128], kt[:], OP.mult))
-    W("v", k_cm)
+    W("v", k_cm, k_nm)
     k1 = inc(v.tensor_tensor(T["cmm"][:], CM, T["msk"][:], OP.mult))
     W("v", k1)
     k2 = inc(v.tensor_tensor(T["lf"][:], T["cmm"][:, 0:16], T["cmm"][:, 16:32], OP.add))

@@ -11,7 +11,8 @@ SCRATCH = {
     "xs": ("dram", [128, 256], "bfloat16"), "xr": ("dram", [128, 256], "bfloat16"),
     "xw": ("sbuf", [128, 2064], "bfloat16"), "xg": ("sbuf", [128, 2048], "bfloat16"),
     "wa": ("sbuf", [128, 2064], "bfloat16"), "wb": ("sbuf", [128, 2064], "bfloat16"), "w4": ("sbuf", [128, 2064], "bfloat16"),
-    "b3": ("sbuf", [128, 2048], "bfloat16"), "rr": ("sbuf", [128, 2048], "bfloat16"),
+    "b3": ("sbuf", [128, 2048], "bfloat16"), "d3": ("sbuf", [128, 512], "bfloat16"), "rr": ("sbuf", [128, 2048], "bfloat16"),
+    "pr2": ("sbuf", [128, 2048], "bfloat16"), "pr3": ("sbuf", [128, 2048], "bfloat16"),
     "lo": ("sbuf", [128, 256], "bfloat16"), "m1": ("sbuf", [128, 256], "bfloat16"), "ip": ("sbuf", [128, 2], "int32"),
     "io8": ("sbuf", [128, 8], "float32"), "pb": ("sbuf", [128, 1], "int32"), "ps": ("sbuf", [128, 1], "int32"),
     "pg": ("sbuf", [128, 1], "int32"),
@@ -19,16 +20,17 @@ SCRATCH = {
     "sf": ("sbuf", [128, 1], "float32"), "mk": ("sbuf", [128, 8], "float32"), "gf": ("sbuf", [128, 1], "float32"),
     "ngf": ("sbuf", [128, 1], "float32"),
     "zz": ("sbuf", [128, 160], "bfloat16"), "on": ("sbuf", [128, 160], "bfloat16"), "half": ("sbuf", [128, 32], "bfloat16"),
-    "basef": ("sbuf", [128, 144], "bfloat16"), "bases": ("sbuf", [128, 144], "bfloat16"), "ids": ("sbuf", [128, 160], "bfloat16"),
+    "basef": ("sbuf", [128, 144], "bfloat16"), "bases": ("sbuf", [128, 144], "bfloat16"), "base0": ("sbuf", [128, 144], "bfloat16"),
+    "ids": ("sbuf", [128, 160], "bfloat16"),
     "bo": ("sbuf", [128, 128], "bfloat16"), "tri": ("sbuf", [128, 128], "bfloat16"), "bo16": ("sbuf", [128, 128], "bfloat16"),
-    "bo32": ("sbuf", [128, 8], "float32"), "kc": ("sbuf", [128, 128], "bfloat16"), "cp": ("sbuf", [128, 128], "bfloat16"),
+    "boh": ("sbuf", [128, 8], "float16"), "kc": ("sbuf", [128, 128], "bfloat16"), "cp": ("sbuf", [128, 128], "bfloat16"),
     "ck": ("sbuf", [128, 128], "bfloat16"), "msk": ("sbuf", [128, 32], "float32"),
     "loi": ("sbuf", [128, 128], "int32"), "nlo": ("sbuf", [128, 144], "bfloat16"), "nhi": ("sbuf", [128, 144], "bfloat16"),
     "kt": ("sbuf", [128, 128], "bfloat16"), "sc1": ("sbuf", [128, 144], "bfloat16"), "sumw": ("sbuf", [128, 144], "float32"),
     "posk": ("sbuf", [128, 144], "bfloat16"), "ai": ("sbuf", [128, 128], "int32"), "a1": ("sbuf", [128, 128], "bfloat16"),
     "bb": ("sbuf", [128, 128], "bfloat16"), "sg": ("sbuf", [128, 128], "bfloat16"), "cmm": ("sbuf", [128, 32], "float32"),
     "lf": ("sbuf", [128, 16], "float32"), "lst": ("sbuf", [128, 16], "uint16"), "oh": ("sbuf", [128, 256], "bfloat16"),
-    "vs": ("sbuf", [128, 256], "float32"), "vh": ("sbuf", [128, 256], "bfloat16"), "vl": ("sbuf", [128, 256], "bfloat16"),
+    "vs": ("sbuf", [128, 256], "float16"), "vh": ("sbuf", [128, 256], "bfloat16"), "vl": ("sbuf", [128, 256], "bfloat16"),
     "yks": ("sbuf", [128, 256], "float32"), "yss": ("sbuf", [128, 256], "float32"),
     "psa": ("psum", [128, 2048], "float32"), "pwa": ("psum", [128, 512], "float32"), "pwb": ("psum", [128, 512], "float32"),
     "px": ("psum", [128, 512], "float32"), "py": ("psum", [128, 512], "float32"),
@@ -37,8 +39,6 @@ for _k in range(1, 6):
     if _k != 2:
         SCRATCH["f%d" % _k] = ("sbuf", [128, 128], "uint16")
     SCRATCH["pt%d" % _k] = ("sbuf", [128, 128], "bfloat16")
-for _k in (0, 2, 3):
-    SCRATCH["pr%d" % _k] = ("sbuf", [128, 2048], "bfloat16")
 NTOK = 126
 SEMAPHORES = (["t%d" % _k for _k in range(NTOK)] + ["anx", "rn", "rf", "rp", "lc", "ax", "af1", "af3", "af4", "af5"]
               + ["ap%d" % _k for _k in range(1, 6)])
@@ -144,7 +144,7 @@ def rank_program(g, core, T, topo):
     k_i = inc(g.iota(T["ip"][:, 0:1], [[0, 1]], 0, 1))
     inc(g.iota(T["io8"][:], [[1, 8]], 0, 0, **small), k_i)
     k_lo = inc(g.iota(T["lo"][:], [[1, 256]], 0, 0, **small))
-    GF = 768
+    GF = 896
     k_fill = inc(g.iota(tab[:, 8192 - GF:8192], [[0, GF]], 8, 0, **small))
 
     k_f0 = inc(v.memset(tab[:, 0:1024], 8.0))
@@ -152,6 +152,7 @@ def rank_program(g, core, T, topo):
     k_f1 = inc(s.activation(tab[:, 1024:2048], tab[:, 0:1024], AF.Copy))
     W("s", k_f1)
     inc(s.activation(tab[:, 2048:4096], tab[:, 0:2048], AF.Copy), k_fill)
+    inc(s.activation(tab[:, 4096:4608], tab[:, 0:512], AF.Copy), k_fill)
 
     k_z = inc(v.memset(T["zz"][:], 0.0))
     W("v", k_i)
@@ -167,7 +168,7 @@ def rank_program(g, core, T, topo):
         inc(v.tensor_scalar(T["vr"][:, 256 * b:256 * b + 256], T["lo"][:], T["ml"][:, 0:1], T["hb"][:, b:b + 1], OP.mult, OP.add), k_vr)
     W("v", l_nx)
     k_n16 = inc(v.tensor_copy(T["nxt16"][:], T["nxi"][:]))
-    inc(v.memset(tab[:, 4096:8192 - GF], 8.0), k_fill)
+    inc(v.memset(tab[:, 4608:8192 - GF], 8.0), k_fill)
     W("v", l_ow)
     k_o16 = inc(v.tensor_copy(T["own16"][:], T["owi"][:]))
     W("v", l_pt)
@@ -175,27 +176,29 @@ def rank_program(g, core, T, topo):
     W("v", k_f0, k_f1, k_fill, k_vr, k_o16)
     k_tab = inc(v.tensor_copy(tab[:, 0:8192].indirect(T["own16"][:, 0:128]), T["vr"][:]))
     W("s", k_vr)
-    k_sz = inc(s.activation(T["xw"][:, 0:2048], T["vr"][:], AF.Copy, scale=0.0))
-    inc(s.activation(T["pr2"][:], T["vr"][:], AF.Copy, scale=0.0), k_sz)
+    k_z4, k_z2, k_za = [inc(s.activation(T[b][:, 0:2048], T["vr"][:], AF.Copy, scale=0.0)) for b in ("w4", "pr2", "wa")]
 
     A, B = helpers(T, topo, core)
     sent = 0
     W("g", k_n16)
-    sent += write(g, T, topo, core, A, T["rln"][:], T["nxt16"][:], "rn")
+    sent += write(g, T, topo, core, A, T["rln"][:], T["nxt16"][:], "rn", 8, 16)
     W("g", k_z)
-    kb = inc(g.affine_select(T["basef"][:], T["zz"][:, 0:144], [[-512, 9], [1, 16]], OP.not_equal, 256.0, -15, 32))
     k_ids = inc(g.affine_select(T["ids"][:], T["zz"][:], [[1, 160]], OP.not_equal, 1.0, -16, -1))
-    W("g", kb)
-    k_bf = inc(g.affine_select(T["basef"][:], T["basef"][:], [[-512, 9], [1, 16]], OP.not_equal, 1.0, -47, 32))
     W("g", k_p0)
-    sent += write(g, T, topo, core, B, T["rlp"][:], T["pt0"][:], "rp")
     sent += writes(g, T, topo, core, [(T.cores[(q - 4) % N], T["pt4"][:], T["pt0"][:], "ap4", 0, 4),
                                       (T.cores[(q - 2) % N], T["pt2"][:], T["pt0"][:], "ap2", 4, 8)])
+    sent += write(g, T, topo, core, B, T["rlp"][:], T["pt0"][:], "rp")
+    kb = inc(g.affine_select(T["basef"][:], T["zz"][:, 0:144], [[-512, 9], [1, 16]], OP.not_equal, 256.0, -15, 32))
+    W("g", kb)
+    k_bf = inc(g.affine_select(T["basef"][:], T["basef"][:], [[-512, 9], [1, 16]], OP.not_equal, 1.0, -47, 32))
     k_on = inc(g.iota(T["on"][:], [[0, 160]], 1, 0, **small))
-    k_c = tok()
-    for name, a, val in (("wa", 2048, -2048), ("wb", 2048, -2048), ("w4", 2048, 0), ("xw", 2048, 8),
-                         ("sumw", 128, 0), ("posk", 128, 0), ("nlo", 128, 0), ("nhi", 128, 0), ("sc1", 0, 0)):
-        inc(g.iota(T[name][:, a:a + 16], [[0, 16]], val, 0, **small), k_c)
+    W("g", k_on)
+    k1 = inc(g.affine_select(T["bases"][:], T["on"][:, 0:144], [[0, 9], [1, 16]], OP.is_equal, 0.0, -15, 0))
+    k_b = inc(g.affine_select(T["base0"][:], T["zz"][:, 0:144], [[-512, 9], [1, 16]], OP.not_equal, 1.0, -79, 32))
+    W("g", k1)
+    k1 = inc(g.affine_select(T["bases"][:], T["bases"][:], [[-16, 9], [0, 16]], OP.is_ge, 0.0, -3, 1))
+    W("g", k1)
+    inc(g.affine_select(T["bases"][:], T["bases"][:], [[16, 9], [0, 16]], OP.is_ge, 0.0, 7, -1), k_b)
 
     def gather2(outb, win, lst):
         ks = []
@@ -213,43 +216,20 @@ def rank_program(g, core, T, topo):
     W("s", k_tab)
     kg = gather2(T["gr"], tab[:, 0:8192], T["nx"])
 
-    psa = T["psa"]
-    freed = [None] * 4
+    pws = (T["pwa"], T["pwb"])
+    pqs = (T["px"], T["py"])
 
-    def row_mm(kk):
-        ks = []
-        for b in range(4):
-            if freed[b]:
-                W("t", freed[b])
-            k = tok()
-            for p in range(4 * b, 4 * b + 4):
-                o = 14 + p - kk
-                inc(t.matmul(psa[:, 128 * p:128 * p + 128], T["ids"][:, o:o + 128], T["pt%d" % kk][:], True, True), k)
-            ks.append(k)
-        return ks
-
-    def row_copy(kk, eng, out, ks):
-        for b in range(4):
-            W(eng, ks[b])
-            c = slice(512 * b, 512 * b + 512)
-            if eng == "v":
-                op = v.tensor_scalar(out[:, c], psa[:, c], T["mk"][:, 2 + kk:3 + kk], None, OP.mult)
-            else:
-                op = s.activation(out[:, c], psa[:, c], AF.Identity, scale=T["mk"][:, 2 + kk:3 + kk])
-            freed[b] = inc(op)
-        return list(freed)
-
-    W("t", k_ids)
-    R("t", "ap4", AP_ENG[4])
-    m4 = row_mm(4)
+    def wrap(pw, base, row, h, first=True, last=True):
+        for p in range(16):
+            op = t.matmul(pw[h][:, 0:64], T[base][:, 15 - p:143 - p], T[row][:, 1024 * h + p:1024 * h + 1024:16],
+                          first and p == 0, last and p == 15)
+        return op
 
     W("t", k_bf)
     kw = []
-    for h, pw in ((0, T["pwa"]), (1, T["pwb"])):
+    for h in range(2):
         W("t", kg[h])
-        for p in range(16):
-            op = t.matmul(pw[:, 0:64], T["basef"][:, 15 - p:143 - p], T["gr"][:, 1024 * h + p:1024 * h + 1024:16], p == 0, p == 15)
-        kw.append(inc(op))
+        kw.append(inc(wrap(pws, "basef", "gr", h)))
 
     k1 = inc(v.tensor_scalar(T["ps"][:], T["ip"][:, 0:1], 15, None, OP.bitwise_and))
     k3 = inc(v.tensor_scalar(T["pg"][:], T["ip"][:, 0:1], 4, 1, OP.arith_shift_right, OP.bitwise_and))
@@ -264,103 +244,129 @@ def rank_program(g, core, T, topo):
     k_nm = inc(v.tensor_scalar(T["msk"][:, 0:16], T["on"][:, 0:16], T["ngf"][:, 0:1], None, OP.mult))
     inc(v.tensor_scalar(T["msk"][:, 16:32], T["on"][:, 0:16], T["gf"][:, 0:1], None, OP.mult), k_nm)
     k_f = tok()
-    for h, pw in ((0, T["pwa"]), (1, T["pwb"])):
+    for h in range(2):
         W("v", kw[h])
-        inc(v.tensor_copy(T["f0"][:, 64 * h:64 * h + 64], pw[:, 0:64]), k_f)
+        inc(v.tensor_copy(T["f0"][:, 64 * h:64 * h + 64], pws[h][:, 0:64]), k_f)
 
     W("g", k_f)
-    sent += write(g, T, topo, core, A, T["rlf"][:], T["f0"][:], "rf")
-    sent += write(g, T, topo, core, T.cores[(q - 4) % N], T["f4"][:], T["f0"][:], "af4")
+    sent += writes(g, T, topo, core, [(A, T["rlf"][:], T["f0"][:], "rf", 8, 16),
+                                      (T.cores[(q - 4) % N], T["f4"][:], T["f0"][:], "af4", 0, 8)])
+    k_c = tok()
+    for name, val in (("w4", 0), ("wa", -2048), ("wb", -2048), ("xw", 8)):
+        inc(g.iota(T[name][:, 2048:2064], [[0, 16]], val, 0, **small), k_c)
+    W("y", k_z4)
+    R("y", "ap4", AP_ENG[4])
+    w4 = inc(g.sync.dma_start(T["w4"][6:128:16, 0:2048], T["pt4"][:]), None, 16)
+    W("y", k_z2, k_p0)
+    k_r2 = inc(g.sync.dma_start(T["pr2"][2:128:16, :], T["pt0"][:]), None, 16)
+    R("y", "ap2", AP_ENG[2])
+    inc(g.sync.dma_start(T["pr2"][4:128:16, :], T["pt2"][:]), k_r2, 16)
     W("y", *kg)
     k_xs = inc(g.sync.dma_start(T["xs"][0:64, :], T["gr"][0:128:16, :]), None, 16)
     inc(g.sync.dma_start(T["xs"][64:128, :], T["gr"][1:128:16, :]), k_xs, 16)
     W("g", k_xs)
     sent += write(g, T, topo, core, T.cores[(q - 2) % N], T["xr"][:], T["xs"][:], "ax")
-    k_z0 = inc(g.iota(T["pr0"][:], [[0, 2048]], 0, 0, **small))
-    W("y", k_sz)
-    R("y", "ap2", AP_ENG[2])
-    k_r2 = inc(g.sync.dma_start(T["pr2"][4:128:16, :], T["pt2"][:]), None, 16)
+    W("y", k_za)
+    R("y", "ap5", AP_ENG[5])
+    w5 = inc(g.sync.dma_start(T["wa"][7:128:16, 0:2048], T["pt5"][:]), None, 16)
+    k_zx = inc(s.activation(T["xw"][:, 0:2048], T["vr"][:], AF.Copy, scale=0.0))
+    W("y", k_zx)
     R("y", "ap1", AP_ENG[1])
     k_xw = inc(g.sync.dma_start(T["xw"][3:128:16, 0:2048], T["pt1"][:]), None, 16)
     R("y", "ax", 8)
     inc(g.sync.dma_start(T["xw"][0:128:16, 0:2048], T["xr"][0:64, :]), k_xw, 16)
     inc(g.sync.dma_start(T["xw"][1:128:16, 0:2048], T["xr"][64:128, :]), k_xw, 16)
-    W("y", k_z0, k_p0)
-    k_r0 = inc(g.sync.dma_start(T["pr0"][2:128:16, :], T["pt0"][:]), None, 16)
 
-    W("s", k_mk)
-    w4 = row_copy(4, "s", T["w4"], m4)
+    psa = T["psa"]
+    W("t", k_ids)
     R("t", "ap3", AP_ENG[3])
-    m3 = row_mm(3)
-    w3 = row_copy(3, "v", T["pr3"], m3)
-    R("t", "ap5", AP_ENG[5])
-    m5 = row_mm(5)
-    w5 = row_copy(5, "s", T["wa"], m5)
+    w3 = []
+    for b in (0, 2, 1, 3):
+        k = tok()
+        for p in range(4 * b, 4 * b + 4):
+            inc(t.matmul(psa[:, 128 * p:128 * p + 128], T["ids"][:, 11 + p:139 + p], T["pt3"][:], True, True), k)
+        c = slice(512 * b, 512 * b + 512)
+        if b < 2:
+            W("v", k)
+            w3.append(inc(v.tensor_scalar(T["pr3"][:, c], psa[:, c], T["mk"][:, 5:6], None, OP.mult)))
+        else:
+            W("s", k, k_mk)
+            w3.append(inc(s.activation(T["pr3"][:, c], psa[:, c], AF.Identity, scale=T["mk"][:, 5:6])))
 
     k3 = inc(v.tensor_scalar(T["loi"][:], T["owi"][:], 255, None, OP.bitwise_and))
     W("v", k3)
     inc(v.tensor_scalar(T["nlo"][:, 0:128], T["loi"][:], 1.0, None, OP.add), k_nm)
     inc(v.tensor_tensor(T["nhi"][:, 0:128], T["owi"][:], T["loi"][:], OP.subtract), k_nm)
 
-    k1 = inc(g.affine_select(T["bases"][:], T["on"][:, 0:144], [[0, 9], [1, 16]], OP.is_equal, 0.0, -15, 0))
-    inc(g.affine_select(T["bo"][:], T["on"][:, 0:128], [[-16, 8], [0, 16]], OP.is_ge, 0.0, 0, 1), k1)
+    k_e = tok()
+    for name, a in (("sumw", 128), ("posk", 128), ("nlo", 128), ("nhi", 128), ("sc1", 0)):
+        inc(g.iota(T[name][:, a:a + 16], [[0, 16]], 0, 0, **small), k_e)
+    k1 = inc(g.affine_select(T["bo"][:], T["on"][:, 0:128], [[-16, 8], [0, 16]], OP.is_ge, 0.0, 0, 1))
     k_kc = inc(g.iota(T["kc"][:], [[0, 8], [1, 16]], 0, 0, **small))
     inc(g.iota(T["m1"][:], [[1, 256]], 1, 0, **small), k_kc)
     W("g", k1)
-    k2 = inc(g.affine_select(T["bases"][:], T["bases"][:], [[-16, 9], [0, 16]], OP.is_ge, 0.0, -2, 1))
-    inc(g.affine_select(T["bo"][:], T["bo"][:], [[16, 8], [0, 16]], OP.is_ge, 0.0, 15, -1), k2)
-    W("g", k2)
-    k_b = inc(g.affine_select(T["bases"][:], T["bases"][:], [[16, 9], [0, 16]], OP.is_ge, 0.0, 7, -1))
-    inc(g.affine_select(T["tri"][:], T["bo"][:], [[1, 128]], OP.is_ge, 0.0, 0, -1), k_b)
+    k_bo = inc(g.affine_select(T["bo"][:], T["bo"][:], [[16, 8], [0, 16]], OP.is_ge, 0.0, 15, -1))
+    W("g", k_bo)
+    inc(g.affine_select(T["tri"][:], T["bo"][:], [[1, 128]], OP.is_ge, 0.0, 0, -1), k_e)
 
     wa, wb = T["wa"], T["wb"]
     R("v", "af4", AF_ENG[4])
-    W("v", k_c, *w4)
-    W("v", *w3)
-    k_b3 = inc(v.tensor_tensor(T["b3"][:], T["w4"][:].indirect(T["f4"][:]), T["pr3"][:], OP.add))
-    SP = 1280
+    W("v", k_c, w4, *w3)
+    k_b3 = inc(v.tensor_tensor(T["b3"][:, 0:1024], T["w4"][:].indirect(T["f4"][:, 0:64]), T["pr3"][:, 0:1024], OP.add))
+    R("s", "af4", AF_ENG[4])
+    W("s", k_c, w4)
+    k1 = inc(s.activation(T["b3"][:, 1024:2048], T["w4"][:].indirect(T["f4"][:, 64:128]), AF.Copy))
+    W("s", k1, *w3)
+    k_b3s = inc(g.scalar.dma_start(T["b3"][5:128:16, 1024:2048], T["pr3"][5:128:16, 1024:2048]), None, 16)
     R("s", "af5", AF_ENG[5])
-    W("s", k_c, *w5)
-    k_d1 = inc(s.activation(wb[:, 0:SP], wa[:].indirect(T["f5"][:, 0:SP // 16]), AF.Copy))
+    W("s", w5)
+    k_d1 = inc(s.activation(wb[:, 0:1024], wa[:].indirect(T["f5"][:, 0:64]), AF.Copy))
     R("v", "af5", AF_ENG[5])
-    W("v", *w5)
-    inc(v.tensor_copy(wb[:, SP:2048], wa[:].indirect(T["f5"][:, SP // 16:128])), k_d1)
+    W("v", w5)
+    inc(v.tensor_copy(wb[:, 1024:2048], wa[:].indirect(T["f5"][:, 64:128])), k_d1)
     W("v", k_d1, k_b3)
-    k_d2 = inc(v.tensor_tensor(wa[:, 0:2048], wb[:].indirect(T["f4"][:]), T["b3"][:], OP.add))
+    k_d2 = inc(v.tensor_tensor(wa[:, 0:1024], wb[:].indirect(T["f4"][:, 0:64]), T["b3"][:, 0:1024], OP.add))
+    W("v", k_b3s)
+    inc(v.tensor_tensor(wa[:, 1024:2048], wb[:].indirect(T["f4"][:, 64:128]), T["b3"][:, 1024:2048], OP.add), k_d2)
     R("v", "af3", AF_ENG[3])
     W("v", k_d2, k_r2)
-    k_d3 = inc(v.tensor_tensor(wb[:, 0:2048], wa[:].indirect(T["f3"][:]), T["pr2"][:], OP.add))
+    SH = 1664
+    X = 2048 - SH
+    k_d3 = inc(v.tensor_tensor(wb[:, 0:SH], wa[:].indirect(T["f3"][:, 0:SH // 16]), T["pr2"][:, 0:SH], OP.add))
 
+    W("t", k_b, k_f, k_r2)
+    for h in range(2):
+        wrap(pws, "base0", "pr2", h, True, False)
+    W("t", *w3)
+    t.matmul(psa[:, 0:X], T["ids"][:, 16:144], T["pr2"][:, SH:2048], True, False)
     R("s", "af1", AF_ENG[1])
     W("s", k_xw)
-    pws = (T["pwa"], T["pwb"])
-    pqs = (T["px"], T["py"])
-    kq, k_xg, k_fg = [], [], tok()
+    kq, k_fg = [], tok()
     for h in range(2):
-        k_xg.append(inc(s.activation(T["xg"][:, 1024 * h:1024 * h + 1024],
-                                     T["xw"][:].indirect(T["f1"][:, 64 * h:64 * h + 64]), AF.Copy)))
-        W("t", k_xg[h])
-        for p in range(16):
-            op = t.matmul(pqs[h][:, 0:64], T["basef"][:, 15 - p:143 - p], T["xg"][:, 1024 * h + p:1024 * h + 1024:16], p == 0, p == 15)
-        kq.append(inc(op))
+        k = inc(s.activation(T["xg"][:, 1024 * h:1024 * h + 1024], T["xw"][:].indirect(T["f1"][:, 64 * h:64 * h + 64]), AF.Copy))
+        W("t", k)
+        kq.append(inc(wrap(pqs, "basef", "xg", h)))
+        if h == 0:
+            wrap(pws, "bases", "xg", 0, False, False)
+    R("s", "af3", AF_ENG[3])
+    W("s", k_d2)
+    k = inc(s.activation(T["d3"][:, 0:X], wa[:].indirect(T["f3"][:, SH // 16:128]), AF.Copy))
+    W("t", k)
+    k = inc(t.matmul(psa[:, 0:X], T["ids"][:, 16:144], T["d3"][:, 0:X], False, True))
+    W("s", k_kc, k_bo)
+    k_sc = inc(s.activation(T["cp"][:], T["kc"][:], AF.Copy, scale=-1.0 / 2048))
+    inc(s.activation(T["ck"][:], T["kc"][:], AF.Copy, scale=-1.0 / 128), k_sc)
+    inc(s.activation(T["bo16"][:], T["bo"][:], AF.Copy, scale=1.0 / 16), k_sc)
+    inc(s.activation(T["half"][:], T["on"][:, 0:32], AF.Copy, scale=0.5), k_sc)
+    W("s", k, k_d1)
+    inc(s.activation(wb[:, SH:2048], psa[:, 0:X], AF.Copy), k_d3)
+    wrap(pws, "bases", "xg", 1, False, False)
     for h in range(2):
         W("v", kq[h])
         inc(v.tensor_copy(T["fg"][:, 64 * h:64 * h + 64], pqs[h][:, 0:64]), k_fg)
 
-    W("s", k_kc, k2)
-    k_sc = inc(s.activation(T["cp"][:], T["kc"][:], AF.Copy, scale=-1.0 / 2048))
-    inc(s.activation(T["ck"][:], T["kc"][:], AF.Copy, scale=-1.0 / 128), k_sc)
-    inc(s.activation(T["bo16"][:], T["bo"][:], AF.Copy, scale=1.0 / 16), k_sc)
-    inc(s.activation(T["bo32"][:], T["bo"][:, 0:128:16], AF.Copy), k_sc)
-    inc(s.activation(T["half"][:], T["on"][:, 0:32], AF.Copy, scale=0.5), k_sc)
-
-    W("t", k_b, k_f, k_r0)
-    for b in ("xg", "pr0"):
-        for h in range(2):
-            for p in range(16):
-                t.matmul(pws[h][:, 0:64], T["bases"][:, 15 - p:143 - p], T[b][:, 1024 * h + p:1024 * h + 1024:16], b == "xg" and p == 0, False)
     T1, T2, T3, CM = psa[:, 0:128], psa[:, 512:640], psa[:, 1024:1152], psa[:, 1536:1568]
-    W("t", k_sc, *w5)
+    W("t", k_sc, k_on)
     t.matmul(T3, T["on"][:, 0:128], T["ck"][:], True, False)
     t.matmul(T2, T["on"][:, 0:128], T["cp"][:], True, False)
 
@@ -370,9 +376,7 @@ def rank_program(g, core, T, topo):
     kw = []
     for h in range(2):
         W("t", kr[h])
-        for p in range(16):
-            op = t.matmul(pws[h][:, 0:64], T["bases"][:, 15 - p:143 - p], T["rr"][:, 1024 * h + p:1024 * h + 1024:16], False, p == 15)
-        kw.append(inc(op))
+        kw.append(inc(wrap(pws, "bases", "rr", h, False, True)))
 
     kt, sc1 = T["kt"], T["sc1"]
     kk_ = []
@@ -385,7 +389,7 @@ def rank_program(g, core, T, topo):
     for h in range(2):
         W("s", kk_[h])
         inc(s.activation(T["sumw"][:, 64 * h:64 * h + 64], pws[h][:, 0:64], AF.Copy), k_sum)
-    W("t", k_scan, k_c, k_fg)
+    W("t", k_scan, k_e, k_fg, k_d3)
     k_t1 = inc(t.matmul(T1, sc1[:, 16:144], T["bo16"][:], True, True))
     k_t3 = inc(t.matmul(T3, sc1[:, 16:144], T["bo16"][:], False, True))
     k_t2 = inc(t.matmul(T2, sc1[:, 16:144], T["bo16"][:], False, True))
@@ -407,20 +411,22 @@ def rank_program(g, core, T, topo):
         k_cm = inc(op, None if a == 0 else k_cm)
     W("v", k_pos)
     k_pk = inc(v.tensor_tensor(T["posk"][:, 0:128], T["px"][:, 0:128], kt[:], OP.mult))
+    W("v", k_bo)
+    k_bh = inc(v.tensor_copy(T["boh"][:], T["bo"][:, 0:128:16]))
     W("v", k_cm, k_nm)
     k1 = inc(v.tensor_tensor(T["cmm"][:], CM, T["msk"][:], OP.mult))
     W("v", k1)
     k2 = inc(v.tensor_tensor(T["lf"][:], T["cmm"][:, 0:16], T["cmm"][:, 16:32], OP.add))
     W("v", k2)
     k3 = inc(v.tensor_scalar(T["lst"][:], T["lf"][:], 64.0, None, OP.add))
-    W("v", k3, k_pk)
+    W("v", k3, k_pk, k_e)
     k_oh = inc(v.tensor_tensor(T["oh"][:], T["posk"][:].indirect(T["lst"][:]), T["m1"][:], OP.is_equal))
     W("v", k_oh, k_sum)
     k_vs = inc(v.tensor_tensor(T["vs"][:], T["sumw"][:].indirect(T["lst"][:]), T["oh"][:], OP.mult))
     k_vh = inc(v.tensor_tensor(T["vh"][:], T["nhi"][:].indirect(T["lst"][:]), T["oh"][:], OP.mult))
     k_vl = inc(v.tensor_tensor(T["vl"][:], T["nlo"][:].indirect(T["lst"][:]), T["oh"][:], OP.mult))
-    W("t", k_vs)
-    k_ys = inc(t.matmul(T["px"][0:8, 0:256], T["bo32"][:], T["vs"][:], True, True))
+    W("t", k_vs, k_bh)
+    k_ys = inc(t.matmul(T["px"][0:8, 0:256], T["boh"][:], T["vs"][:], True, True))
     W("t", k_vh)
     t.matmul(T["py"][0:8, 0:256], T["bo"][:, 0:128:16], T["vh"][:], True, False)
     W("t", k_vl)

@@ -4,24 +4,24 @@ from concourse.mybir import AluOpType as OP, ActivationFunctionType as AF
 SCRATCH = {
     "nx": ("sbuf", [128, 128], "uint16"),
     "rln": ("sbuf", [128, 128], "uint16"), "rlf": ("sbuf", [128, 128], "uint16"), "rlp": ("sbuf", [128, 128], "bfloat16"),
+    "rlq": ("dram", [128, 128], "bfloat16"),
     "owi": ("sbuf", [128, 128], "int32"), "nxi": ("sbuf", [128, 128], "int32"), "pti": ("sbuf", [128, 128], "int32"),
     "own16": ("sbuf", [128, 128], "uint16"), "nxt16": ("sbuf", [128, 128], "uint16"), "pt0": ("sbuf", [128, 128], "bfloat16"),
     "tab": ("sbuf", [128, 8192], "bfloat16"), "vr": ("sbuf", [128, 2048], "bfloat16"), "gr": ("sbuf", [128, 2048], "bfloat16"),
     "f0": ("sbuf", [128, 128], "uint16"), "fg": ("sbuf", [128, 128], "uint16"),
     "xs": ("dram", [128, 256], "bfloat16"), "xr": ("dram", [128, 256], "bfloat16"),
+    "xp": ("dram", [128, 128], "bfloat16"), "pq5": ("dram", [128, 128], "bfloat16"), "pq3": ("dram", [128, 128], "bfloat16"),
     "xw": ("sbuf", [128, 2064], "bfloat16"), "xg": ("sbuf", [128, 2048], "bfloat16"),
-    "wa": ("sbuf", [128, 2064], "bfloat16"), "wb": ("sbuf", [128, 2064], "bfloat16"), "w4": ("sbuf", [128, 2064], "bfloat16"),
-    "b3": ("sbuf", [128, 2048], "bfloat16"), "d3": ("sbuf", [128, 512], "bfloat16"), "rr": ("sbuf", [128, 2048], "bfloat16"),
-    "pr2": ("sbuf", [128, 2048], "bfloat16"), "pr3": ("sbuf", [128, 2048], "bfloat16"),
+    "w5": ("sbuf", [128, 2064], "bfloat16"), "wd": ("sbuf", [128, 2064], "bfloat16"), "wb": ("sbuf", [128, 2064], "bfloat16"),
+    "d3": ("sbuf", [128, 512], "bfloat16"), "rr": ("sbuf", [128, 2048], "bfloat16"), "pr2": ("sbuf", [128, 2048], "bfloat16"),
     "lo": ("sbuf", [128, 256], "bfloat16"), "m1": ("sbuf", [128, 256], "bfloat16"), "ip": ("sbuf", [128, 2], "int32"),
-    "io8": ("sbuf", [128, 8], "float32"), "pb": ("sbuf", [128, 1], "int32"), "ps": ("sbuf", [128, 1], "int32"),
+    "io8": ("sbuf", [128, 8], "float32"), "pb": ("sbuf", [128, 1], "int32"),
     "pg": ("sbuf", [128, 1], "int32"),
     "ml": ("sbuf", [128, 1], "float32"), "nml": ("sbuf", [128, 1], "float32"), "hb": ("sbuf", [128, 8], "float32"),
-    "sf": ("sbuf", [128, 1], "float32"), "mk": ("sbuf", [128, 8], "float32"), "gf": ("sbuf", [128, 1], "float32"),
-    "ngf": ("sbuf", [128, 1], "float32"),
+    "gf": ("sbuf", [128, 1], "float32"), "ngf": ("sbuf", [128, 1], "float32"),
     "zz": ("sbuf", [128, 160], "bfloat16"), "on": ("sbuf", [128, 160], "bfloat16"), "half": ("sbuf", [128, 32], "bfloat16"),
     "basef": ("sbuf", [128, 144], "bfloat16"), "bases": ("sbuf", [128, 144], "bfloat16"), "base0": ("sbuf", [128, 144], "bfloat16"),
-    "ids": ("sbuf", [128, 160], "bfloat16"),
+    "ids": ("sbuf", [128, 128], "bfloat16"),
     "bo": ("sbuf", [128, 128], "bfloat16"), "tri": ("sbuf", [128, 128], "bfloat16"), "bo16": ("sbuf", [128, 128], "bfloat16"),
     "boh": ("sbuf", [128, 8], "float16"), "kc": ("sbuf", [128, 128], "bfloat16"), "cp": ("sbuf", [128, 128], "bfloat16"),
     "ck": ("sbuf", [128, 128], "bfloat16"), "msk": ("sbuf", [128, 32], "float32"),
@@ -35,15 +35,16 @@ SCRATCH = {
     "psa": ("psum", [128, 2048], "float32"), "pwa": ("psum", [128, 512], "float32"), "pwb": ("psum", [128, 512], "float32"),
     "px": ("psum", [128, 512], "float32"), "py": ("psum", [128, 512], "float32"),
 }
-for _k in range(1, 6):
-    if _k != 2:
-        SCRATCH["f%d" % _k] = ("sbuf", [128, 128], "uint16")
+for _k in (1, 3, 4):
+    SCRATCH["f%d" % _k] = ("sbuf", [128, 128], "uint16")
+for _k in (1, 2, 4):
     SCRATCH["pt%d" % _k] = ("sbuf", [128, 128], "bfloat16")
-NTOK = 126
-SEMAPHORES = (["t%d" % _k for _k in range(NTOK)] + ["anx", "rn", "rf", "rp", "lc", "ax", "af1", "af3", "af4", "af5"]
-              + ["ap%d" % _k for _k in range(1, 6)])
+NTOK = 130
+SEMAPHORES = (["t%d" % _k for _k in range(NTOK)] + ["anx", "rn", "rf", "rp", "rq", "lc", "ax", "af1", "af3", "af4", "aq3", "aq5"]
+              + ["ap1", "ap2", "ap4"])
 
 ODD = (5, 3, 1)
+NONE = -2048
 
 
 def engs(topo, src, dst, a, b):
@@ -88,20 +89,16 @@ def hand_on(g, core, T, topo):
             g.wait_ge(T.sem["rn"], 8)
             sent += write(g, T, topo, core, T.cores[(q + 1) % N], T["nx"][:], T["rln"][:], "anx")
             g.wait_ge(T.sem["rf"], 8)
-            sent += write(g, T, topo, core, T.cores[(q - 5) % N], T["f5"][:], T["rlf"][:], "af5")
-            sent += writes(g, T, topo, core, [(T.cores[(q - 3) % N], T["f3"][:], T["rlf"][:], "af3", 0, 4),
-                                              (T.cores[(q - 1) % N], T["f1"][:], T["rlf"][:], "af1", 4, 8)])
+            sent += write(g, T, topo, core, T.cores[(q - 1) % N], T["f1"][:], T["rlf"][:], "af1")
+            sent += write(g, T, topo, core, T.cores[(q - 3) % N], T["f3"][:], T["rlf"][:], "af3")
         elif core == B:
             g.wait_ge(T.sem["rp"], 8)
-            sent += writes(g, T, topo, core, [(T.cores[(q - 5) % N], T["pt5"][:], T["rlp"][:], "ap5", 0, 4),
-                                              (T.cores[(q - 3) % N], T["pt3"][:], T["rlp"][:], "ap3", 4, 6),
-                                              (T.cores[(q - 1) % N], T["pt1"][:], T["rlp"][:], "ap1", 6, 8)])
+            sent += write(g, T, topo, core, T.cores[(q - 1) % N], T["pt1"][:], T["rlp"][:], "ap1")
+            g.wait_ge(T.sem["rq"], 4)
+            sent += write(g, T, topo, core, T.cores[(q - 5) % N], T["pq5"][:], T["rlq"][:], "aq5")
+            sent += write(g, T, topo, core, T.cores[(q - 3) % N], T["pq3"][:], T["rlq"][:], "aq3")
         if sent:
             g.wait_ge(T.sem["lc"], sent)
-
-
-AF_ENG = {5: 8, 4: 8, 3: 4, 1: 4}
-AP_ENG = {5: 4, 4: 4, 3: 2, 2: 4, 1: 2}
 
 
 def rank_program(g, core, T, topo):
@@ -136,27 +133,30 @@ def rank_program(g, core, T, topo):
             seen[(queue, sem)] = n
             Q[queue].wait_ge(T.sem[sem], n)
 
-    l_nx = inc(g.sync.dma_start(T["nxi"][:], T.nxt[:]), None, 16)
-    l_ow = inc(g.scalar.dma_start(T["owi"][:], T.own[:]), None, 16)
+    l_ow = inc(g.sync.dma_start(T["owi"][:], T.own[:]), None, 16)
+    l_nx = inc(g.scalar.dma_start(T["nxi"][:], T.nxt[:]), None, 16)
     l_pt = inc(g.sync.dma_start(T["pti"][:], T.pts[:]), None, 16)
 
     tab = T["tab"]
     k_i = inc(g.iota(T["ip"][:, 0:1], [[0, 1]], 0, 1))
     inc(g.iota(T["io8"][:], [[1, 8]], 0, 0, **small), k_i)
     k_lo = inc(g.iota(T["lo"][:], [[1, 256]], 0, 0, **small))
-    GF = 896
-    k_fill = inc(g.iota(tab[:, 8192 - GF:8192], [[0, GF]], 8, 0, **small))
+    k_fill = inc(g.iota(tab[:, 7168:8192], [[0, 1024]], NONE, 0, **small))
 
-    k_f0 = inc(v.memset(tab[:, 0:1024], 8.0))
+    k_f0 = inc(v.memset(tab[:, 0:512], float(NONE)))
+    k_f1 = inc(v.memset(tab[:, 512:1024], float(NONE)))
+    W("y", k_f0, k_f1)
+    k_fd = inc(g.sync.dma_start(tab[:, 3840:4864], tab[:, 0:1024]), None, 16)
     W("s", k_f0)
-    k_f1 = inc(s.activation(tab[:, 1024:2048], tab[:, 0:1024], AF.Copy))
+    k_f2 = inc(s.activation(tab[:, 1024:1536], tab[:, 0:512], AF.Copy))
     W("s", k_f1)
-    inc(s.activation(tab[:, 2048:4096], tab[:, 0:2048], AF.Copy), k_fill)
-    inc(s.activation(tab[:, 4096:4608], tab[:, 0:512], AF.Copy), k_fill)
+    inc(s.activation(tab[:, 1536:2560], tab[:, 0:1024], AF.Copy), k_fill)
+    W("s", k_f2)
+    inc(s.activation(tab[:, 2560:3840], tab[:, 0:1280], AF.Copy), k_fill)
 
     k_z = inc(v.memset(T["zz"][:], 0.0))
     W("v", k_i)
-    k1 = inc(v.tensor_scalar(T["pb"][:], T["ip"][:, 0:1], 1, None, OP.bitwise_and))
+    k1 = inc(v.tensor_scalar(T["pb"][:], T["ip"][:, 0:1], 3, 1, OP.arith_shift_right, OP.bitwise_and))
     W("v", k1)
     k2 = inc(v.tensor_copy(T["ml"][:], T["pb"][:]))
     k3 = inc(v.tensor_scalar(T["nml"][:], T["pb"][:], -1.0, 1.0, OP.mult, OP.add))
@@ -166,35 +166,40 @@ def rank_program(g, core, T, topo):
     k_vr = tok()
     for b in range(8):
         inc(v.tensor_scalar(T["vr"][:, 256 * b:256 * b + 256], T["lo"][:], T["ml"][:, 0:1], T["hb"][:, b:b + 1], OP.mult, OP.add), k_vr)
-    W("v", l_nx)
-    k_n16 = inc(v.tensor_copy(T["nxt16"][:], T["nxi"][:]))
-    inc(v.memset(tab[:, 4608:8192 - GF], 8.0), k_fill)
-    W("v", l_ow)
-    k_o16 = inc(v.tensor_copy(T["own16"][:], T["owi"][:]))
     W("v", l_pt)
     k_p0 = inc(v.tensor_copy(T["pt0"][:], T["pti"][:]))
-    W("v", k_f0, k_f1, k_fill, k_vr, k_o16)
+    W("y", k_vr, k_p0)
+    k_vp = inc(g.sync.dma_start(T["vr"][4:128:16, :], T["pt0"][:]), None, 16)
+    W("v", l_nx)
+    k_n16 = inc(v.tensor_copy(T["nxt16"][:], T["nxi"][:]))
+    inc(v.memset(tab[:, 4864:7168], float(NONE)), k_fill)
+    W("v", l_ow)
+    k_o16 = inc(v.tensor_copy(T["own16"][:], T["owi"][:]))
+    W("v", k_f0, k_f1, k_f2, k_fill, k_fd, k_vp, k_o16)
     k_tab = inc(v.tensor_copy(tab[:, 0:8192].indirect(T["own16"][:, 0:128]), T["vr"][:]))
-    W("s", k_vr)
-    k_z4, k_z2, k_za = [inc(s.activation(T[b][:, 0:2048], T["vr"][:], AF.Copy, scale=0.0)) for b in ("w4", "pr2", "wa")]
+    W("s", k_vp)
+    k_zx = inc(s.activation(T["xw"][:, 16:2064], T["vr"][:], AF.Copy, scale=0.0))
 
     A, B = helpers(T, topo, core)
     sent = 0
     W("g", k_n16)
     sent += write(g, T, topo, core, A, T["rln"][:], T["nxt16"][:], "rn", 8, 16)
     W("g", k_z)
-    k_ids = inc(g.affine_select(T["ids"][:], T["zz"][:], [[1, 160]], OP.not_equal, 1.0, -16, -1))
+    kb = inc(g.affine_select(T["basef"][:], T["zz"][:, 0:144], [[-512, 9], [1, 16]], OP.not_equal, 256.0, -15, 32))
     W("g", k_p0)
     sent += writes(g, T, topo, core, [(T.cores[(q - 4) % N], T["pt4"][:], T["pt0"][:], "ap4", 0, 4),
                                       (T.cores[(q - 2) % N], T["pt2"][:], T["pt0"][:], "ap2", 4, 8)])
-    sent += write(g, T, topo, core, B, T["rlp"][:], T["pt0"][:], "rp")
-    kb = inc(g.affine_select(T["basef"][:], T["zz"][:, 0:144], [[-512, 9], [1, 16]], OP.not_equal, 256.0, -15, 32))
+    sent += write(g, T, topo, core, B, T["rlp"][:], T["pt0"][:], "rp", 8, 16)
     W("g", kb)
-    k_bf = inc(g.affine_select(T["basef"][:], T["basef"][:], [[-512, 9], [1, 16]], OP.not_equal, 1.0, -47, 32))
+    k_bf = inc(g.affine_select(T["basef"][:], T["basef"][:], [[-512, 9], [1, 16]], OP.not_equal, 1.0, -271, 32))
+    k_c = tok()
+    for name in ("xw", "w5", "wd", "wb"):
+        inc(g.iota(T[name][:, 0:16], [[0, 16]], NONE, 0, **small), k_c)
+    k_b = inc(g.affine_select(T["base0"][:], T["zz"][:, 0:144], [[-512, 9], [1, 16]], OP.not_equal, 1.0, -143, 32))
     k_on = inc(g.iota(T["on"][:], [[0, 160]], 1, 0, **small))
     W("g", k_on)
     k1 = inc(g.affine_select(T["bases"][:], T["on"][:, 0:144], [[0, 9], [1, 16]], OP.is_equal, 0.0, -15, 0))
-    k_b = inc(g.affine_select(T["base0"][:], T["zz"][:, 0:144], [[-512, 9], [1, 16]], OP.not_equal, 1.0, -79, 32))
+    k_ids = inc(g.affine_select(T["ids"][:], T["zz"][:, 0:128], [[1, 128]], OP.not_equal, 1.0, 0, -1))
     W("g", k1)
     k1 = inc(g.affine_select(T["bases"][:], T["bases"][:], [[-16, 9], [0, 16]], OP.is_ge, 0.0, -3, 1))
     W("g", k1)
@@ -216,6 +221,11 @@ def rank_program(g, core, T, topo):
     W("s", k_tab)
     kg = gather2(T["gr"], tab[:, 0:8192], T["nx"])
 
+    W("y", *kg)
+    k_xp = inc(g.sync.dma_start(T["xp"][:], T["gr"][4:128:16, :]), None, 16)
+    W("s", *kg)
+    k_xs = inc(g.scalar.dma_start(T["xs"][:], T["gr"][0:128:8, :]), None, 16)
+
     pws = (T["pwa"], T["pwb"])
     pqs = (T["px"], T["py"])
 
@@ -225,74 +235,57 @@ def rank_program(g, core, T, topo):
                           first and p == 0, last and p == 15)
         return op
 
+    def lists(out, h, kws, k):
+        W("v", kws[h])
+        inc(v.tensor_scalar(T[out][:, 64 * h:64 * h + 64], pqs[h][:, 0:64], 16.0, 0.0, OP.add, OP.max), k)
+
     W("t", k_bf)
     kw = []
     for h in range(2):
         W("t", kg[h])
-        kw.append(inc(wrap(pws, "basef", "gr", h)))
+        kw.append(inc(wrap(pqs, "basef", "gr", h)))
 
-    k1 = inc(v.tensor_scalar(T["ps"][:], T["ip"][:, 0:1], 15, None, OP.bitwise_and))
+    k_f, k_z5 = tok(), tok()
+    inc(v.memset(T["w5"][:, 16:1040], 0.0), k_z5)
+    lists("f0", 0, kw, k_f)
+    inc(v.memset(T["w5"][:, 1040:2064], 0.0), k_z5)
+    lists("f0", 1, kw, k_f)
+    k_z2 = inc(s.activation(T["pr2"][:], T["vr"][:], AF.Copy, scale=0.0))
+
+    W("g", k_xs)
+    sent += write(g, T, topo, core, T.cores[(q - 2) % N], T["xr"][:], T["xs"][:], "ax")
+    W("g", k_f, k_xp)
+    sent += writes(g, T, topo, core, [(A, T["rlf"][:], T["f0"][:], "rf", 8, 16),
+                                      (B, T["rlq"][:], T["xp"][:], "rq", 4, 8),
+                                      (T.cores[(q - 4) % N], T["f4"][:], T["f0"][:], "af4", 0, 4)])
+
+    W("y", k_zx)
+    R("y", "ap1", 8)
+    k_xw = inc(g.sync.dma_start(T["xw"][3:128:16, 16:2064], T["pt1"][:]), None, 16)
+    W("y", k_z5)
+    R("y", "ap4", 4)
+    k_w5 = inc(g.sync.dma_start(T["w5"][6:128:16, 16:2064], T["pt4"][:]), None, 16)
+    W("y", k_z2)
+    R("y", "ap2", 4)
+    k_r2 = inc(g.sync.dma_start(T["pr2"][4:128:16, :], T["pt2"][:]), None, 16)
+    R("y", "ax", 8)
+    inc(g.sync.dma_start(T["xw"][0:128:8, 16:2064], T["xr"][:]), k_xw, 16)
+    R("y", "aq5", 8)
+    inc(g.sync.dma_start(T["w5"][7:128:16, 16:2064], T["pq5"][:]), k_w5, 16)
+    R("y", "aq3", 8)
+    inc(g.sync.dma_start(T["pr2"][5:128:16, :], T["pq3"][:]), k_r2, 16)
+
+    W("t", k_b, k_vp)
+    for h in range(2):
+        wrap(pws, "base0", "vr", h, True, False)
+
     k3 = inc(v.tensor_scalar(T["pg"][:], T["ip"][:, 0:1], 4, 1, OP.arith_shift_right, OP.bitwise_and))
-    W("v", k1)
-    k2 = inc(v.tensor_copy(T["sf"][:], T["ps"][:]))
-    W("v", k2)
-    k_mk = inc(v.tensor_scalar(T["mk"][:], T["io8"][:], T["sf"][:, 0:1], None, OP.is_equal))
     W("v", k3)
     k2 = inc(v.tensor_copy(T["gf"][:], T["pg"][:]))
     inc(v.tensor_scalar(T["ngf"][:], T["pg"][:], -1.0, 1.0, OP.mult, OP.add), k2)
     W("v", k2, k_on)
     k_nm = inc(v.tensor_scalar(T["msk"][:, 0:16], T["on"][:, 0:16], T["ngf"][:, 0:1], None, OP.mult))
     inc(v.tensor_scalar(T["msk"][:, 16:32], T["on"][:, 0:16], T["gf"][:, 0:1], None, OP.mult), k_nm)
-    k_f = tok()
-    for h in range(2):
-        W("v", kw[h])
-        inc(v.tensor_copy(T["f0"][:, 64 * h:64 * h + 64], pws[h][:, 0:64]), k_f)
-
-    W("g", k_f)
-    sent += writes(g, T, topo, core, [(A, T["rlf"][:], T["f0"][:], "rf", 8, 16),
-                                      (T.cores[(q - 4) % N], T["f4"][:], T["f0"][:], "af4", 0, 8)])
-    k_c = tok()
-    for name, val in (("w4", 0), ("wa", -2048), ("wb", -2048), ("xw", 8)):
-        inc(g.iota(T[name][:, 2048:2064], [[0, 16]], val, 0, **small), k_c)
-    W("y", k_z4)
-    R("y", "ap4", AP_ENG[4])
-    w4 = inc(g.sync.dma_start(T["w4"][6:128:16, 0:2048], T["pt4"][:]), None, 16)
-    W("y", k_z2, k_p0)
-    k_r2 = inc(g.sync.dma_start(T["pr2"][2:128:16, :], T["pt0"][:]), None, 16)
-    R("y", "ap2", AP_ENG[2])
-    inc(g.sync.dma_start(T["pr2"][4:128:16, :], T["pt2"][:]), k_r2, 16)
-    W("y", *kg)
-    k_xs = inc(g.sync.dma_start(T["xs"][0:64, :], T["gr"][0:128:16, :]), None, 16)
-    inc(g.sync.dma_start(T["xs"][64:128, :], T["gr"][1:128:16, :]), k_xs, 16)
-    W("g", k_xs)
-    sent += write(g, T, topo, core, T.cores[(q - 2) % N], T["xr"][:], T["xs"][:], "ax")
-    W("y", k_za)
-    R("y", "ap5", AP_ENG[5])
-    w5 = inc(g.sync.dma_start(T["wa"][7:128:16, 0:2048], T["pt5"][:]), None, 16)
-    k_zx = inc(s.activation(T["xw"][:, 0:2048], T["vr"][:], AF.Copy, scale=0.0))
-    W("y", k_zx)
-    R("y", "ap1", AP_ENG[1])
-    k_xw = inc(g.sync.dma_start(T["xw"][3:128:16, 0:2048], T["pt1"][:]), None, 16)
-    R("y", "ax", 8)
-    inc(g.sync.dma_start(T["xw"][0:128:16, 0:2048], T["xr"][0:64, :]), k_xw, 16)
-    inc(g.sync.dma_start(T["xw"][1:128:16, 0:2048], T["xr"][64:128, :]), k_xw, 16)
-
-    psa = T["psa"]
-    W("t", k_ids)
-    R("t", "ap3", AP_ENG[3])
-    w3 = []
-    for b in (0, 2, 1, 3):
-        k = tok()
-        for p in range(4 * b, 4 * b + 4):
-            inc(t.matmul(psa[:, 128 * p:128 * p + 128], T["ids"][:, 11 + p:139 + p], T["pt3"][:], True, True), k)
-        c = slice(512 * b, 512 * b + 512)
-        if b < 2:
-            W("v", k)
-            w3.append(inc(v.tensor_scalar(T["pr3"][:, c], psa[:, c], T["mk"][:, 5:6], None, OP.mult)))
-        else:
-            W("s", k, k_mk)
-            w3.append(inc(s.activation(T["pr3"][:, c], psa[:, c], AF.Identity, scale=T["mk"][:, 5:6])))
-
     k3 = inc(v.tensor_scalar(T["loi"][:], T["owi"][:], 255, None, OP.bitwise_and))
     W("v", k3)
     inc(v.tensor_scalar(T["nlo"][:, 0:128], T["loi"][:], 1.0, None, OP.add), k_nm)
@@ -303,67 +296,51 @@ def rank_program(g, core, T, topo):
         inc(g.iota(T[name][:, a:a + 16], [[0, 16]], 0, 0, **small), k_e)
     k1 = inc(g.affine_select(T["bo"][:], T["on"][:, 0:128], [[-16, 8], [0, 16]], OP.is_ge, 0.0, 0, 1))
     k_kc = inc(g.iota(T["kc"][:], [[0, 8], [1, 16]], 0, 0, **small))
-    inc(g.iota(T["m1"][:], [[1, 256]], 1, 0, **small), k_kc)
     W("g", k1)
     k_bo = inc(g.affine_select(T["bo"][:], T["bo"][:], [[16, 8], [0, 16]], OP.is_ge, 0.0, 15, -1))
+    inc(g.iota(T["m1"][:], [[1, 256]], 1, 0, **small), k_kc)
     W("g", k_bo)
     inc(g.affine_select(T["tri"][:], T["bo"][:], [[1, 128]], OP.is_ge, 0.0, 0, -1), k_e)
 
-    wa, wb = T["wa"], T["wb"]
-    R("v", "af4", AF_ENG[4])
-    W("v", k_c, w4, *w3)
-    k_b3 = inc(v.tensor_tensor(T["b3"][:, 0:1024], T["w4"][:].indirect(T["f4"][:, 0:64]), T["pr3"][:, 0:1024], OP.add))
-    R("s", "af4", AF_ENG[4])
-    W("s", k_c, w4)
-    k1 = inc(s.activation(T["b3"][:, 1024:2048], T["w4"][:].indirect(T["f4"][:, 64:128]), AF.Copy))
-    W("s", k1, *w3)
-    k_b3s = inc(g.scalar.dma_start(T["b3"][5:128:16, 1024:2048], T["pr3"][5:128:16, 1024:2048]), None, 16)
-    R("s", "af5", AF_ENG[5])
-    W("s", w5)
-    k_d1 = inc(s.activation(wb[:, 0:1024], wa[:].indirect(T["f5"][:, 0:64]), AF.Copy))
-    R("v", "af5", AF_ENG[5])
-    W("v", w5)
-    inc(v.tensor_copy(wb[:, 1024:2048], wa[:].indirect(T["f5"][:, 64:128])), k_d1)
-    W("v", k_d1, k_b3)
-    k_d2 = inc(v.tensor_tensor(wa[:, 0:1024], wb[:].indirect(T["f4"][:, 0:64]), T["b3"][:, 0:1024], OP.add))
-    W("v", k_b3s)
-    inc(v.tensor_tensor(wa[:, 1024:2048], wb[:].indirect(T["f4"][:, 64:128]), T["b3"][:, 1024:2048], OP.add), k_d2)
-    R("v", "af3", AF_ENG[3])
-    W("v", k_d2, k_r2)
-    SH = 1664
-    X = 2048 - SH
-    k_d3 = inc(v.tensor_tensor(wb[:, 0:SH], wa[:].indirect(T["f3"][:, 0:SH // 16]), T["pr2"][:, 0:SH], OP.add))
-
-    W("t", k_b, k_f, k_r2)
-    for h in range(2):
-        wrap(pws, "base0", "pr2", h, True, False)
-    W("t", *w3)
-    t.matmul(psa[:, 0:X], T["ids"][:, 16:144], T["pr2"][:, SH:2048], True, False)
-    R("s", "af1", AF_ENG[1])
-    W("s", k_xw)
+    w5, wd, wb = T["w5"], T["wd"], T["wb"]
+    for x in "vs":
+        R(x, "af1", 8)
+        W(x, k_c, k_xw)
+    kx = gather2(T["xg"], T["xw"][:], T["f1"])
+    W("t", k_f)
     kq, k_fg = [], tok()
     for h in range(2):
-        k = inc(s.activation(T["xg"][:, 1024 * h:1024 * h + 1024], T["xw"][:].indirect(T["f1"][:, 64 * h:64 * h + 64]), AF.Copy))
-        W("t", k)
+        W("t", kx[h])
         kq.append(inc(wrap(pqs, "basef", "xg", h)))
-        if h == 0:
-            wrap(pws, "bases", "xg", 0, False, False)
-    R("s", "af3", AF_ENG[3])
-    W("s", k_d2)
-    k = inc(s.activation(T["d3"][:, 0:X], wa[:].indirect(T["f3"][:, SH // 16:128]), AF.Copy))
-    W("t", k)
-    k = inc(t.matmul(psa[:, 0:X], T["ids"][:, 16:144], T["d3"][:, 0:X], False, True))
+    for x in "vs":
+        R(x, "af4", 4)
+        W(x, k_w5)
+    k_d2 = inc(v.tensor_copy(wd[:, 16:1040], w5[:].indirect(T["f4"][:, 0:64])))
+    inc(s.activation(wd[:, 1040:2064], w5[:].indirect(T["f4"][:, 64:128]), AF.Copy), k_d2)
+    for h in range(2):
+        lists("fg", h, kq, k_fg)
+    SH = 1600
+    X = 2048 - SH
+    psa = T["psa"]
+    for x in "vs":
+        R(x, "af3", 8)
+        W(x, k_d2)
+    W("v", k_r2)
+    k_d3 = inc(v.tensor_tensor(wb[:, 16:16 + SH], wd[:].indirect(T["f3"][:, 0:SH // 16]), T["pr2"][:, 0:SH], OP.add))
+    ks = inc(s.activation(T["d3"][:, 0:X], wd[:].indirect(T["f3"][:, SH // 16:128]), AF.Copy))
+    W("t", k_ids, k_r2)
+    t.matmul(psa[:, 0:X], T["ids"][:], T["pr2"][:, SH:2048], True, False)
+    wrap(pws, "bases", "xg", 0, False, False)
+    W("t", ks)
+    kp = inc(t.matmul(psa[:, 0:X], T["ids"][:], T["d3"][:, 0:X], False, True))
+    wrap(pws, "bases", "xg", 1, False, False)
     W("s", k_kc, k_bo)
     k_sc = inc(s.activation(T["cp"][:], T["kc"][:], AF.Copy, scale=-1.0 / 2048))
     inc(s.activation(T["ck"][:], T["kc"][:], AF.Copy, scale=-1.0 / 128), k_sc)
     inc(s.activation(T["bo16"][:], T["bo"][:], AF.Copy, scale=1.0 / 16), k_sc)
     inc(s.activation(T["half"][:], T["on"][:, 0:32], AF.Copy, scale=0.5), k_sc)
-    W("s", k, k_d1)
-    inc(s.activation(wb[:, SH:2048], psa[:, 0:X], AF.Copy), k_d3)
-    wrap(pws, "bases", "xg", 1, False, False)
-    for h in range(2):
-        W("v", kq[h])
-        inc(v.tensor_copy(T["fg"][:, 64 * h:64 * h + 64], pqs[h][:, 0:64]), k_fg)
+    W("s", kp)
+    inc(s.activation(wb[:, 16 + SH:2064], psa[:, 0:X], AF.Copy), k_d3)
 
     T1, T2, T3, CM = psa[:, 0:128], psa[:, 512:640], psa[:, 1024:1152], psa[:, 1536:1568]
     W("t", k_sc, k_on)

from concourse.bass import DstId, RemoteDMATransfer
from concourse.mybir import AluOpType as OP, ActivationFunctionType as AF

SCRATCH = {
    "nx": ("sbuf", [128, 128], "uint16"),
    "rln": ("sbuf", [128, 128], "uint16"), "rlf": ("sbuf", [128, 128], "uint16"), "rlp": ("sbuf", [128, 128], "bfloat16"),
    "rlq": ("dram", [128, 128], "bfloat16"),
    "owi": ("sbuf", [128, 128], "int32"), "nxi": ("sbuf", [128, 128], "int32"), "pti": ("sbuf", [128, 128], "int32"),
    "own16": ("sbuf", [128, 128], "uint16"), "nxt16": ("sbuf", [128, 128], "uint16"), "pt0": ("sbuf", [128, 128], "bfloat16"),
    "tab": ("sbuf", [128, 8192], "bfloat16"), "vr": ("sbuf", [128, 2048], "bfloat16"), "gr": ("sbuf", [128, 2048], "bfloat16"),
    "f0": ("sbuf", [128, 128], "uint16"), "fg": ("sbuf", [128, 128], "uint16"),
    "xs": ("dram", [128, 256], "bfloat16"), "xr": ("dram", [128, 256], "bfloat16"),
    "xp": ("dram", [128, 128], "bfloat16"), "pq5": ("dram", [128, 128], "bfloat16"), "pq3": ("dram", [128, 128], "bfloat16"),
    "xw": ("sbuf", [128, 2064], "bfloat16"), "xg": ("sbuf", [128, 2048], "bfloat16"),
    "w5": ("sbuf", [128, 2064], "bfloat16"), "wd": ("sbuf", [128, 2064], "bfloat16"), "wb": ("sbuf", [128, 2064], "bfloat16"),
    "d3": ("sbuf", [128, 512], "bfloat16"), "rr": ("sbuf", [128, 2048], "bfloat16"), "pr2": ("sbuf", [128, 2048], "bfloat16"),
    "lo": ("sbuf", [128, 256], "bfloat16"), "m1": ("sbuf", [128, 256], "bfloat16"), "ip": ("sbuf", [128, 2], "int32"),
    "io8": ("sbuf", [128, 8], "float32"), "pb": ("sbuf", [128, 1], "int32"),
    "pg": ("sbuf", [128, 1], "int32"),
    "ml": ("sbuf", [128, 1], "float32"), "nml": ("sbuf", [128, 1], "float32"), "hb": ("sbuf", [128, 8], "float32"),
    "gf": ("sbuf", [128, 1], "float32"), "ngf": ("sbuf", [128, 1], "float32"),
    "zz": ("sbuf", [128, 160], "bfloat16"), "on": ("sbuf", [128, 160], "bfloat16"), "half": ("sbuf", [128, 32], "bfloat16"),
    "basef": ("sbuf", [128, 144], "bfloat16"), "bases": ("sbuf", [128, 144], "bfloat16"), "base0": ("sbuf", [128, 144], "bfloat16"),
    "ids": ("sbuf", [128, 128], "bfloat16"),
    "bo": ("sbuf", [128, 128], "bfloat16"), "tri": ("sbuf", [128, 128], "bfloat16"), "bo16": ("sbuf", [128, 128], "bfloat16"),
    "boh": ("sbuf", [128, 8], "float16"), "kc": ("sbuf", [128, 128], "bfloat16"), "cp": ("sbuf", [128, 128], "bfloat16"),
    "ck": ("sbuf", [128, 128], "bfloat16"), "msk": ("sbuf", [128, 32], "float32"),
    "loi": ("sbuf", [128, 128], "int32"), "nlo": ("sbuf", [128, 144], "bfloat16"), "nhi": ("sbuf", [128, 144], "bfloat16"),
    "kt": ("sbuf", [128, 128], "bfloat16"), "sc1": ("sbuf", [128, 144], "bfloat16"), "sumw": ("sbuf", [128, 144], "float32"),
    "posk": ("sbuf", [128, 144], "bfloat16"), "ai": ("sbuf", [128, 128], "int32"), "a1": ("sbuf", [128, 128], "bfloat16"),
    "bb": ("sbuf", [128, 128], "bfloat16"), "sg": ("sbuf", [128, 128], "bfloat16"), "cmm": ("sbuf", [128, 32], "float32"),
    "lf": ("sbuf", [128, 16], "float32"), "lst": ("sbuf", [128, 16], "uint16"), "oh": ("sbuf", [128, 256], "bfloat16"),
    "vs": ("sbuf", [128, 256], "float16"), "vh": ("sbuf", [128, 256], "bfloat16"), "vl": ("sbuf", [128, 256], "bfloat16"),
    "yks": ("sbuf", [128, 256], "float32"), "yss": ("sbuf", [128, 256], "float32"),
    "psa": ("psum", [128, 2048], "float32"), "pwa": ("psum", [128, 512], "float32"), "pwb": ("psum", [128, 512], "float32"),
    "px": ("psum", [128, 512], "float32"), "py": ("psum", [128, 512], "float32"),
}
for _k in (1, 3, 4):
    SCRATCH["f%d" % _k] = ("sbuf", [128, 128], "uint16")
for _k in (1, 2, 4):
    SCRATCH["pt%d" % _k] = ("sbuf", [128, 128], "bfloat16")
NTOK = 130
SEMAPHORES = (["t%d" % _k for _k in range(NTOK)] + ["anx", "rn", "rf", "rp", "rq", "lc", "ax", "af1", "af3", "af4", "aq3", "aq5"]
              + ["ap1", "ap2", "ap4"])

ODD = (5, 3, 1)
NONE = -2048


def engs(topo, src, dst, a, b):
    e = topo.engines(src, dst)[a:b]
    return sum(1 << x for x in e), len(e)


def write(g, T, topo, src, dst, out, in_, sem, a=0, b=8):
    rid, pid = topo.addr(dst, src)
    m, k = engs(topo, src, dst, a, b)
    g.remote_dma(out, in_, T.sem[sem], T.sem["lc"], pid, rid, m)
    return k


def writes(g, T, topo, src, parts):
    tr, n = [], 0
    for dst, out, in_, sem, a, b in parts:
        rid, pid = topo.addr(dst, src)
        m, k = engs(topo, src, dst, a, b)
        n += k
        tr.append(RemoteDMATransfer(dst_ids=[DstId(rid=rid, pnc=pid)], dma_engine_mask=m, remote_sem=T.sem[sem], src=in_, dst=out))
    g.remote_dma_fused(tr, local_sem=T.sem["lc"])
    return n


def helpers(T, topo, rc):
    q, N = T.rank_of(rc), len(T.cores)
    far = [T.cores[(q + 1) % N]] + [T.cores[(q - k) % N] for k in ODD]
    c = [x for x in topo.cores_of(rc) if x != rc and topo.die(x) == topo.die(rc) and all(topo.may_write(x, d) for d in far)]
    return c[0], c[1]


def hand_on(g, core, T, topo):
    N = len(T.cores)
    for rc in T.cores:
        if rc not in topo.cores_of(core):
            continue
        q = T.rank_of(rc)
        A, B = helpers(T, topo, rc)
        sent = 0
        if core == A:
            g.wait_ge(T.sem["rn"], 8)
            sent += write(g, T, topo, core, T.cores[(q + 1) % N], T["nx"][:], T["rln"][:], "anx")
            g.wait_ge(T.sem["rf"], 8)
            sent += write(g, T, topo, core, T.cores[(q - 1) % N], T["f1"][:], T["rlf"][:], "af1")
            sent += write(g, T, topo, core, T.cores[(q - 3) % N], T["f3"][:], T["rlf"][:], "af3")
        elif core == B:
            g.wait_ge(T.sem["rp"], 8)
            sent += write(g, T, topo, core, T.cores[(q - 1) % N], T["pt1"][:], T["rlp"][:], "ap1")
            g.wait_ge(T.sem["rq"], 4)
            sent += write(g, T, topo, core, T.cores[(q - 5) % N], T["pq5"][:], T["rlq"][:], "aq5")
            sent += write(g, T, topo, core, T.cores[(q - 3) % N], T["pq3"][:], T["rlq"][:], "aq3")
        if sent:
            g.wait_ge(T.sem["lc"], sent)


def rank_program(g, core, T, topo):
    q = T.rank_of(core)
    if q is None:
        hand_on(g, core, T, topo)
        return
    N = len(T.cores)
    Q = {"g": g, "v": g.vector, "s": g.scalar, "t": g.tensor, "y": g.sync}
    v, s, t = g.vector, g.scalar, g.tensor
    used, seen = [0], {}
    small = {"allow_small_or_imprecise_dtypes": True}

    def tok():
        used[0] += 1
        return [T.sem["t%d" % (used[0] - 1)], 0, used[0] - 1]

    def inc(op, k=None, n=1):
        k = k or tok()
        op.then_inc(k[0], n)
        k[1] += n
        return k

    def W(queue, *toks):
        for k in toks:
            if seen.get((queue, k[2]), -1) < k[1]:
                seen[(queue, k[2])] = k[1]
                Q[queue].wait_ge(k[0], k[1])

    def R(queue, sem, n):
        if (queue, sem) not in seen:
            seen[(queue, sem)] = n
            Q[queue].wait_ge(T.sem[sem], n)

    l_ow = inc(g.sync.dma_start(T["owi"][:], T.own[:]), None, 16)
    l_nx = inc(g.scalar.dma_start(T["nxi"][:], T.nxt[:]), None, 16)
    l_pt = inc(g.sync.dma_start(T["pti"][:], T.pts[:]), None, 16)

    tab = T["tab"]
    k_i = inc(g.iota(T["ip"][:, 0:1], [[0, 1]], 0, 1))
    inc(g.iota(T["io8"][:], [[1, 8]], 0, 0, **small), k_i)
    k_lo = inc(g.iota(T["lo"][:], [[1, 256]], 0, 0, **small))
    k_fill = inc(g.iota(tab[:, 7168:8192], [[0, 1024]], NONE, 0, **small))

    k_f0 = inc(v.memset(tab[:, 0:512], float(NONE)))
    k_f1 = inc(v.memset(tab[:, 512:1024], float(NONE)))
    W("y", k_f0, k_f1)
    k_fd = inc(g.sync.dma_start(tab[:, 3840:4864], tab[:, 0:1024]), None, 16)
    W("s", k_f0)
    k_f2 = inc(s.activation(tab[:, 1024:1536], tab[:, 0:512], AF.Copy))
    W("s", k_f1)
    inc(s.activation(tab[:, 1536:2560], tab[:, 0:1024], AF.Copy), k_fill)
    W("s", k_f2)
    inc(s.activation(tab[:, 2560:3840], tab[:, 0:1280], AF.Copy), k_fill)

    k_z = inc(v.memset(T["zz"][:], 0.0))
    W("v", k_i)
    k1 = inc(v.tensor_scalar(T["pb"][:], T["ip"][:, 0:1], 3, 1, OP.arith_shift_right, OP.bitwise_and))
    W("v", k1)
    k2 = inc(v.tensor_copy(T["ml"][:], T["pb"][:]))
    k3 = inc(v.tensor_scalar(T["nml"][:], T["pb"][:], -1.0, 1.0, OP.mult, OP.add))
    W("v", k3)
    inc(v.tensor_scalar(T["hb"][:], T["io8"][:], T["nml"][:, 0:1], None, OP.mult), k2)
    W("v", k2, k_lo)
    k_vr = tok()
    for b in range(8):
        inc(v.tensor_scalar(T["vr"][:, 256 * b:256 * b + 256], T["lo"][:], T["ml"][:, 0:1], T["hb"][:, b:b + 1], OP.mult, OP.add), k_vr)
    W("v", l_pt)
    k_p0 = inc(v.tensor_copy(T["pt0"][:], T["pti"][:]))
    W("y", k_vr, k_p0)
    k_vp = inc(g.sync.dma_start(T["vr"][4:128:16, :], T["pt0"][:]), None, 16)
    W("v", l_nx)
    k_n16 = inc(v.tensor_copy(T["nxt16"][:], T["nxi"][:]))
    inc(v.memset(tab[:, 4864:7168], float(NONE)), k_fill)
    W("v", l_ow)
    k_o16 = inc(v.tensor_copy(T["own16"][:], T["owi"][:]))
    W("v", k_f0, k_f1, k_f2, k_fill, k_fd, k_vp, k_o16)
    k_tab = inc(v.tensor_copy(tab[:, 0:8192].indirect(T["own16"][:, 0:128]), T["vr"][:]))
    W("s", k_vp)
    k_zx = inc(s.activation(T["xw"][:, 16:2064], T["vr"][:], AF.Copy, scale=0.0))

    A, B = helpers(T, topo, core)
    sent = 0
    W("g", k_n16)
    sent += write(g, T, topo, core, A, T["rln"][:], T["nxt16"][:], "rn", 8, 16)
    W("g", k_z)
    kb = inc(g.affine_select(T["basef"][:], T["zz"][:, 0:144], [[-512, 9], [1, 16]], OP.not_equal, 256.0, -15, 32))
    W("g", k_p0)
    sent += writes(g, T, topo, core, [(T.cores[(q - 4) % N], T["pt4"][:], T["pt0"][:], "ap4", 0, 4),
                                      (T.cores[(q - 2) % N], T["pt2"][:], T["pt0"][:], "ap2", 4, 8)])
    sent += write(g, T, topo, core, B, T["rlp"][:], T["pt0"][:], "rp", 8, 16)
    W("g", kb)
    k_bf = inc(g.affine_select(T["basef"][:], T["basef"][:], [[-512, 9], [1, 16]], OP.not_equal, 1.0, -271, 32))
    k_c = tok()
    for name in ("xw", "w5", "wd", "wb"):
        inc(g.iota(T[name][:, 0:16], [[0, 16]], NONE, 0, **small), k_c)
    k_b = inc(g.affine_select(T["base0"][:], T["zz"][:, 0:144], [[-512, 9], [1, 16]], OP.not_equal, 1.0, -143, 32))
    k_on = inc(g.iota(T["on"][:], [[0, 160]], 1, 0, **small))
    W("g", k_on)
    k1 = inc(g.affine_select(T["bases"][:], T["on"][:, 0:144], [[0, 9], [1, 16]], OP.is_equal, 0.0, -15, 0))
    k_ids = inc(g.affine_select(T["ids"][:], T["zz"][:, 0:128], [[1, 128]], OP.not_equal, 1.0, 0, -1))
    W("g", k1)
    k1 = inc(g.affine_select(T["bases"][:], T["bases"][:], [[-16, 9], [0, 16]], OP.is_ge, 0.0, -3, 1))
    W("g", k1)
    inc(g.affine_select(T["bases"][:], T["bases"][:], [[16, 9], [0, 16]], OP.is_ge, 0.0, 7, -1), k_b)

    def gather2(outb, win, lst):
        ks = []
        for h in range(2):
            k = tok()
            a = 1024 * h
            inc(v.tensor_copy(outb[:, a:a + 512], win.indirect(lst[:, a // 16:a // 16 + 32])), k)
            inc(s.activation(outb[:, a + 512:a + 1024], win.indirect(lst[:, a // 16 + 32:a // 16 + 64]), AF.Copy), k)
            ks.append(k)
        return ks

    R("v", "anx", 8)
    R("s", "anx", 8)
    W("v", k_tab)
    W("s", k_tab)
    kg = gather2(T["gr"], tab[:, 0:8192], T["nx"])

    W("y", *kg)
    k_xp = inc(g.sync.dma_start(T["xp"][:], T["gr"][4:128:16, :]), None, 16)
    W("s", *kg)
    k_xs = inc(g.scalar.dma_start(T["xs"][:], T["gr"][0:128:8, :]), None, 16)

    pws = (T["pwa"], T["pwb"])
    pqs = (T["px"], T["py"])

    def wrap(pw, base, row, h, first=True, last=True):
        for p in range(16):
            op = t.matmul(pw[h][:, 0:64], T[base][:, 15 - p:143 - p], T[row][:, 1024 * h + p:1024 * h + 1024:16],
                          first and p == 0, last and p == 15)
        return op

    def lists(out, h, kws, k):
        W("v", kws[h])
        inc(v.tensor_scalar(T[out][:, 64 * h:64 * h + 64], pqs[h][:, 0:64], 16.0, 0.0, OP.add, OP.max), k)

    W("t", k_bf)
    kw = []
    for h in range(2):
        W("t", kg[h])
        kw.append(inc(wrap(pqs, "basef", "gr", h)))

    k_f, k_z5 = tok(), tok()
    inc(v.memset(T["w5"][:, 16:1040], 0.0), k_z5)
    lists("f0", 0, kw, k_f)
    inc(v.memset(T["w5"][:, 1040:2064], 0.0), k_z5)
    lists("f0", 1, kw, k_f)
    k_z2 = inc(s.activation(T["pr2"][:], T["vr"][:], AF.Copy, scale=0.0))

    W("g", k_xs)
    sent += write(g, T, topo, core, T.cores[(q - 2) % N], T["xr"][:], T["xs"][:], "ax")
    W("g", k_f, k_xp)
    sent += writes(g, T, topo, core, [(A, T["rlf"][:], T["f0"][:], "rf", 8, 16),
                                      (B, T["rlq"][:], T["xp"][:], "rq", 4, 8),
                                      (T.cores[(q - 4) % N], T["f4"][:], T["f0"][:], "af4", 0, 4)])

    W("y", k_zx)
    R("y", "ap1", 8)
    k_xw = inc(g.sync.dma_start(T["xw"][3:128:16, 16:2064], T["pt1"][:]), None, 16)
    W("y", k_z5)
    R("y", "ap4", 4)
    k_w5 = inc(g.sync.dma_start(T["w5"][6:128:16, 16:2064], T["pt4"][:]), None, 16)
    W("y", k_z2)
    R("y", "ap2", 4)
    k_r2 = inc(g.sync.dma_start(T["pr2"][4:128:16, :], T["pt2"][:]), None, 16)
    R("y", "ax", 8)
    inc(g.sync.dma_start(T["xw"][0:128:8, 16:2064], T["xr"][:]), k_xw, 16)
    R("y", "aq5", 8)
    inc(g.sync.dma_start(T["w5"][7:128:16, 16:2064], T["pq5"][:]), k_w5, 16)
    R("y", "aq3", 8)
    inc(g.sync.dma_start(T["pr2"][5:128:16, :], T["pq3"][:]), k_r2, 16)

    W("t", k_b, k_vp)
    for h in range(2):
        wrap(pws, "base0", "vr", h, True, False)

    k3 = inc(v.tensor_scalar(T["pg"][:], T["ip"][:, 0:1], 4, 1, OP.arith_shift_right, OP.bitwise_and))
    W("v", k3)
    k2 = inc(v.tensor_copy(T["gf"][:], T["pg"][:]))
    inc(v.tensor_scalar(T["ngf"][:], T["pg"][:], -1.0, 1.0, OP.mult, OP.add), k2)
    W("v", k2, k_on)
    k_nm = inc(v.tensor_scalar(T["msk"][:, 0:16], T["on"][:, 0:16], T["ngf"][:, 0:1], None, OP.mult))
    inc(v.tensor_scalar(T["msk"][:, 16:32], T["on"][:, 0:16], T["gf"][:, 0:1], None, OP.mult), k_nm)
    k3 = inc(v.tensor_scalar(T["loi"][:], T["owi"][:], 255, None, OP.bitwise_and))
    W("v", k3)
    inc(v.tensor_scalar(T["nlo"][:, 0:128], T["loi"][:], 1.0, None, OP.add), k_nm)
    inc(v.tensor_tensor(T["nhi"][:, 0:128], T["owi"][:], T["loi"][:], OP.subtract), k_nm)

    k_e = tok()
    for name, a in (("sumw", 128), ("posk", 128), ("nlo", 128), ("nhi", 128), ("sc1", 0)):
        inc(g.iota(T[name][:, a:a + 16], [[0, 16]], 0, 0, **small), k_e)
    k1 = inc(g.affine_select(T["bo"][:], T["on"][:, 0:128], [[-16, 8], [0, 16]], OP.is_ge, 0.0, 0, 1))
    k_kc = inc(g.iota(T["kc"][:], [[0, 8], [1, 16]], 0, 0, **small))
    W("g", k1)
    k_bo = inc(g.affine_select(T["bo"][:], T["bo"][:], [[16, 8], [0, 16]], OP.is_ge, 0.0, 15, -1))
    inc(g.iota(T["m1"][:], [[1, 256]], 1, 0, **small), k_kc)
    W("g", k_bo)
    inc(g.affine_select(T["tri"][:], T["bo"][:], [[1, 128]], OP.is_ge, 0.0, 0, -1), k_e)

    w5, wd, wb = T["w5"], T["wd"], T["wb"]
    for x in "vs":
        R(x, "af1", 8)
        W(x, k_c, k_xw)
    kx = gather2(T["xg"], T["xw"][:], T["f1"])
    W("t", k_f)
    kq, k_fg = [], tok()
    for h in range(2):
        W("t", kx[h])
        kq.append(inc(wrap(pqs, "basef", "xg", h)))
    for x in "vs":
        R(x, "af4", 4)
        W(x, k_w5)
    k_d2 = inc(v.tensor_copy(wd[:, 16:1040], w5[:].indirect(T["f4"][:, 0:64])))
    inc(s.activation(wd[:, 1040:2064], w5[:].indirect(T["f4"][:, 64:128]), AF.Copy), k_d2)
    for h in range(2):
        lists("fg", h, kq, k_fg)
    SH = 1600
    X = 2048 - SH
    psa = T["psa"]
    for x in "vs":
        R(x, "af3", 8)
        W(x, k_d2)
    W("v", k_r2)
    k_d3 = inc(v.tensor_tensor(wb[:, 16:16 + SH], wd[:].indirect(T["f3"][:, 0:SH // 16]), T["pr2"][:, 0:SH], OP.add))
    ks = inc(s.activation(T["d3"][:, 0:X], wd[:].indirect(T["f3"][:, SH // 16:128]), AF.Copy))
    W("t", k_ids, k_r2)
    t.matmul(psa[:, 0:X], T["ids"][:], T["pr2"][:, SH:2048], True, False)
    wrap(pws, "bases", "xg", 0, False, False)
    W("t", ks)
    kp = inc(t.matmul(psa[:, 0:X], T["ids"][:], T["d3"][:, 0:X], False, True))
    wrap(pws, "bases", "xg", 1, False, False)
    W("s", k_kc, k_bo)
    k_sc = inc(s.activation(T["cp"][:], T["kc"][:], AF.Copy, scale=-1.0 / 2048))
    inc(s.activation(T["ck"][:], T["kc"][:], AF.Copy, scale=-1.0 / 128), k_sc)
    inc(s.activation(T["bo16"][:], T["bo"][:], AF.Copy, scale=1.0 / 16), k_sc)
    inc(s.activation(T["half"][:], T["on"][:, 0:32], AF.Copy, scale=0.5), k_sc)
    W("s", kp)
    inc(s.activation(wb[:, 16 + SH:2064], psa[:, 0:X], AF.Copy), k_d3)

    T1, T2, T3, CM = psa[:, 0:128], psa[:, 512:640], psa[:, 1024:1152], psa[:, 1536:1568]
    W("t", k_sc, k_on)
    t.matmul(T3, T["on"][:, 0:128], T["ck"][:], True, False)
    t.matmul(T2, T["on"][:, 0:128], T["cp"][:], True, False)

    W("v", k_d3, k_fg)
    W("s", k_d3, k_fg)
    kr = gather2(T["rr"], wb[:], T["fg"])
    kw = []
    for h in range(2):
        W("t", kr[h])
        kw.append(inc(wrap(pws, "bases", "rr", h, False, True)))

    kt, sc1 = T["kt"], T["sc1"]
    kk_ = []
    for h in range(2):
        W("v", kw[h])
        kk_.append(inc(v.tensor_scalar(kt[:, 64 * h:64 * h + 64], pws[h][:, 0:64], 0.0, None, OP.is_ge)))
    W("v", *kk_)
    k_scan = inc(v.tensor_tensor_scan(sc1[:, 16:144], kt[:], kt[:], 0.0, OP.add, OP.max))
    k_sum = tok()
    for h in range(2):
        W("s", kk_[h])
        inc(s.activation(T["sumw"][:, 64 * h:64 * h + 64], pws[h][:, 0:64], AF.Copy), k_sum)
    W("t", k_scan, k_e, k_fg, k_d3)
    k_t1 = inc(t.matmul(T1, sc1[:, 16:144], T["bo16"][:], True, True))
    k_t3 = inc(t.matmul(T3, sc1[:, 16:144], T["bo16"][:], False, True))
    k_t2 = inc(t.matmul(T2, sc1[:, 16:144], T["bo16"][:], False, True))
    t.matmul(T["px"][:, 0:128], T["bo"][:], sc1[:, 15:143], True, False)
    k_pos = inc(t.matmul(T["px"][:, 0:128], T["tri"][:], kt[:], False, True))
    W("v", k_t1)
    k_a = inc(v.tensor_scalar(T["ai"][:], T1, -0.46875, None, OP.add))
    W("s", k_t3)
    k_sg = inc(s.activation(T["sg"][:], T3, AF.Sign, bias=-0.03125, scale=-1.0))
    W("v", k_a, k_t2)
    k_ab = inc(v.tensor_tensor(T["a1"][:], T2, T["ai"][:], OP.is_le))
    W("v", k_kc)
    inc(v.tensor_tensor(T["bb"][:], T["ai"][:], T["kc"][:], OP.is_equal), k_ab)
    W("t", k_sg, k_ab)
    for a in range(4):
        c = slice(32 * a, 32 * a + 32)
        t.matmul(psa[c, 1536:1568], T["half"][:], T["sg"][:, c], True, False)
        op = t.matmul(psa[c, 1536:1568], T["a1"][:, c], T["bb"][:, c], False, True)
        k_cm = inc(op, None if a == 0 else k_cm)
    W("v", k_pos)
    k_pk = inc(v.tensor_tensor(T["posk"][:, 0:128], T["px"][:, 0:128], kt[:], OP.mult))
    W("v", k_bo)
    k_bh = inc(v.tensor_copy(T["boh"][:], T["bo"][:, 0:128:16]))
    W("v", k_cm, k_nm)
    k1 = inc(v.tensor_tensor(T["cmm"][:], CM, T["msk"][:], OP.mult))
    W("v", k1)
    k2 = inc(v.tensor_tensor(T["lf"][:], T["cmm"][:, 0:16], T["cmm"][:, 16:32], OP.add))
    W("v", k2)
    k3 = inc(v.tensor_scalar(T["lst"][:], T["lf"][:], 64.0, None, OP.add))
    W("v", k3, k_pk, k_e)
    k_oh = inc(v.tensor_tensor(T["oh"][:], T["posk"][:].indirect(T["lst"][:]), T["m1"][:], OP.is_equal))
    W("v", k_oh, k_sum)
    k_vs = inc(v.tensor_tensor(T["vs"][:], T["sumw"][:].indirect(T["lst"][:]), T["oh"][:], OP.mult))
    k_vh = inc(v.tensor_tensor(T["vh"][:], T["nhi"][:].indirect(T["lst"][:]), T["oh"][:], OP.mult))
    k_vl = inc(v.tensor_tensor(T["vl"][:], T["nlo"][:].indirect(T["lst"][:]), T["oh"][:], OP.mult))
    W("t", k_vs, k_bh)
    k_ys = inc(t.matmul(T["px"][0:8, 0:256], T["boh"][:], T["vs"][:], True, True))
    W("t", k_vh)
    t.matmul(T["py"][0:8, 0:256], T["bo"][:, 0:128:16], T["vh"][:], True, False)
    W("t", k_vl)
    k_yk = inc(t.matmul(T["py"][0:8, 0:256], T["bo"][:, 0:128:16], T["vl"][:], False, True))
    W("s", k_ys)
    k1 = inc(s.activation(T["yss"][0:8, :], T["px"][0:8, 0:256], AF.Copy))
    W("s", k1)
    o1 = inc(g.scalar.dma_start(T.ys[:], T["yss"][0:8, :]), None, 16)
    W("v", k_yk)
    k2 = inc(v.tensor_scalar(T["yks"][0:8, :], T["py"][0:8, 0:256], -1.0, None, OP.add))
    W("y", k2)
    o2 = inc(g.sync.dma_start(T.yk[:], T["yks"][0:8, :]), None, 16)
    W("s", o1)
    W("y", o2)
    g.wait_ge(T.sem["lc"], sent)
